import numpy as np, ml_dtypes
CORES = [1,5,17,21,33,37,49,53]
N = 8
BF = ml_dtypes.bfloat16
def gentries(a):
    return np.ascontiguousarray(a.reshape(8, 16, -1).transpose(0, 2, 1)).reshape(8, -1)
def gtable(e):
    e = np.asarray(e); return np.ascontiguousarray(e.reshape(8, -1, 16).transpose(0, 2, 1)).reshape(128, -1).astype(np.int32)
V, GH, RO, DF, TR, FQ = 4096, 128, 6, 12, 11, 3
NS, NU = V // 16, V // 256; S = NS + NU + 1; W = V + (N - 1) * GH
LO, HI = DF + 2, 2 * DF + 1
SMALL = (0, 0, 1, 2, 3, 7, 14, 15, 16)
def parts(rng, share):
    x = rng.integers(LO, HI + 1, (N, 8, 16, V)); xb = rng.integers(LO, HI + 1, (N, 8, 16, V))
    a = np.where(rng.random((N, 8, V)) < share, rng.integers(V, W, (N, 8, V)), rng.integers(0, V, (N, 8, V)))
    return x, xb, a, np.zeros((N, 8, S), np.int64), np.full((N, 8, S), 16, np.int64)
def tame(a):
    k = np.where(a >= V, (a - V) % GH, 0)
    return np.where(a >= V, a - k + k % 14, np.where((a == 14) | (a == 15), 0, a))
def pack(x, xb, a, sg, lm):
    return {"x0": np.ascontiguousarray(x.reshape(N, 128, V)).astype(np.float32).astype(BF), "xi": np.ascontiguousarray(xb.reshape(N, 128, V)).astype(np.float32).astype(BF),
            "ad": np.stack([gtable(e) for e in a]), "sg": np.asarray(sg).astype(np.int32), "lm": np.asarray(lm).astype(np.int32)}
def lows(rng, x, xb, a, n):
    o = rng.permutation(V)[:n]; t = rng.choice(np.array([TR - 1, TR, TR + 1, 16, 16]), n)
    m = np.argsort(rng.random((16, n)), axis=0) < t
    x[:, o] = np.where(m, rng.integers(0, 4, (16, n)), x[:, o]); xb[:, o] = np.where(m, rng.integers(0, 4, (16, n)), xb[:, o])
    h = n // 2; a[o[:h]] = np.where(rng.random(h) < 0.5, o[:h], rng.permutation(o[:h]))
def trigger(rng, x, a, sg, lm):
    s = NS - 1 if rng.random() < 0.5 else int(rng.integers(1, NS))
    lm[:NS] = rng.choice(np.array([13, 14, 16]), NS); lm[s] = rng.integers(0, 5); lm[NS + s // 16] = 0; lm[S - 1] = 0
    for i in range(5):
        v = 16 * s + 3 * i; e = rng.integers(0, 4, 16)
        x[:, v + 2] = e; x[:, v + 1] = e + DF; x[:, v] = e + 2 * DF; a[v] = v + 1; a[v + 1] = v + 2; a[v + 2] = v + 2
    a[16 * s + 15] = 16 * s + 15
def plant(rng, x, xb, a, cr, mode, keep, near):
    x[:, 15] = 2; xb[:, 15] = 2; x[:, 14] = LO; xb[:, 14] = LO; a[14:16] = 15
    if mode == 2: x[:, 15] = LO; x[:, 14] = 1; xb[:, 14] = 1; a[14:16] = 14
    to = 14 if mode == 3 else 15
    o = np.flatnonzero(cr); n = len(o); t = rng.choice(np.array([TR, TR, TR + 1, 16]), n)
    st = np.where(np.argsort(rng.random((16, n)), axis=0) < t, rng.integers(LO + 1, HI + 1, (16, n)), LO)
    x[:, o] = st; xb[:, o] = st if keep else LO; a[o] = to
    o = rng.permutation(np.flatnonzero(~cr[16:]) + 16)[:near]; n = len(o)
    x[:, o] = np.where(np.argsort(rng.random((16, n)), axis=0) < TR - 1, rng.integers(LO + 1, HI + 1, (16, n)), LO); a[o] = to
    if mode == 2: xb[:, o] = x[:, o]
def strike(rng, x, a, lm, s, t):
    n = (1, 1, 2, 3, 5, 8, 13)[t - 1]
    a[(a >> 4) == s] = 0; v = 16 * s + np.arange(16); a[v] = v
    p = 16 * s + rng.permutation(16)[:n + 1]; e = rng.integers(0, 4, 16)
    x[:, p] = (e + DF)[:, None]; x[:, p[0]] = e + 2 * DF; x[:, p[n]] = e; a[p[:n]] = p[1:]
    lm[s] = 0; lm[NS + s // 16] = 0; lm[S - 1] = 0
def setup_inputs(rng):
    x, xb, a, sg, lm = parts(rng, 0.06); order = rng.permutation(N)
    mix = ((0.9, 0.07, 0.03), (0.75, 0.15, 0.1), (0.95, 0.03, 0.02), (0.6, 0.25, 0.15))
    for q in range(N):
        n = FQ if q == order[0] else FQ - 1 if q == order[1] else int(rng.integers(0, FQ - 1))
        weak = rng.permutation(8)[:n]
        for g in range(8):
            sg[q, g] = rng.choice(3, S, p=mix[int(rng.integers(0, 4))])
            lm[q, g, :NS] = rng.choice(np.array([3, 4, 6, 8, 10, 13, 16]), NS); lm[q, g, NS:NS + NU] = rng.choice(np.array([1, 2, 4, 8, 16]), NU)
            lows(rng, x[q, g], xb[q, g], a[q, g], (V // 512, V // 128, V // 64)[int(rng.integers(0, 3))])
            if np.any(weak == g): trigger(rng, x[q, g], a[q, g], sg[q, g], lm[q, g])
    return pack(x, xb, a, sg, lm)
def setup_inputs_spread(rng):
    x, xb, a, sg, lm = parts(rng, 0.12)
    x = np.minimum((np.exp2(6 * rng.random((N, 8, 1, V))) * rng.random((N, 8, 16, V))).astype(np.int64), 63)
    xb = np.minimum((np.exp2(6 * rng.random((N, 8, 1, V))) * rng.random((N, 8, 16, V))).astype(np.int64), 63)
    for q in range(N):
        o = rng.permutation(8); k = rng.permutation(8)[:FQ - 1]
        for i in range(8):
            g = int(o[i])
            if i % 2: a[q, g] = np.where(a[q, g] < V, (V * rng.random(V) ** 3).astype(np.int64), a[q, g])
            if i < 4: sg[q, g] = rng.choice(3, S, p=(0.97, 0.02, 0.01))
            else: sg[q, g] = rng.choice(3, S, p=(0.6, 0.25, 0.15)); lm[q, g, :S - 1] = rng.integers(0, 17, S - 1)
            if np.any(k == g): lm[q, g, S - 1] = rng.integers(0, 4)
    return pack(x, xb, a, sg, lm)
def setup_inputs_ends(rng):
    x, xb, a, sg, lm = parts(rng, 0.15)
    def both():
        t = rng.choice(np.array([0, 0, TR - 1, TR, TR + 1, 16, 16]), (N, 8, V, 1))
        return np.ascontiguousarray((63 * (np.argsort(rng.random((N, 8, V, 16)), axis=3) < t)).transpose(0, 1, 3, 2))
    x = both(); xb = both()
    u = rng.random((N, 8, V)); a = np.where(u < 0.36, 0, np.where(u < 0.72, W - 1, a))
    z = 63 * rng.integers(0, 2, (N, 8, 1)); z[:, 7] = 0; x[..., 0] = z; xb[..., 0] = z
    sg = 2 * (rng.random((N, 8, S)) < rng.choice(np.array([0.1, 0.5]), (N, 8, 1))).astype(np.int64)
    lm = 16 * (rng.random((N, 8, S)) < rng.choice(np.array([0.5, 0.9]), (N, 8, 1))).astype(np.int64)
    lm[..., S - 1] = 16; sg[..., S - 1] = 2 * (rng.random((N, 8)) < 0.25)
    x[:, 7, :, V - 16:] = 63; xb[:, 7, :, V - 16:] = 63; a[:, 7, V - 16:] = 0; a[:, 7, 0] = 0; lm[:, 7, NS - 1] = 16
    for q in range(N):
        k = rng.permutation(7)[:FQ if q == N - 1 else FQ - 1]
        for g in k:
            lm[q, g, S - 1] = 0
            if q == N - 1:
                lm[q, g, NS:NS + NU] = 0; x[q, g, :, 0] = 0; xb[q, g] = 0; xb[q, g, :, V - 16:] = 63
                u = rng.random(V); a[q, g] = np.where(u < 0.86, 0, np.where(u < 0.93, V - 1, rng.integers(0, V, V)))
                a[q, g, 0] = 0; a[q, g, V - 16:] = V - 1
    return pack(x, xb, a, sg, lm)
def pair(rng, die, top):
    if die:
        c = int(rng.integers(0, top)); return c, (top if rng.random() < 0.3 else c + 1)
    c = SMALL[int(rng.integers(0, 9))]; return c, min(c if rng.random() < 0.5 else 0, top)
def setup_inputs_corners(rng):
    x, xb, a, sg, lm = parts(rng, 0.05); a = tame(a); sg = rng.integers(0, 3, (N, 8, S)); order = rng.permutation(N); more = int(rng.integers(FQ + 1, 8))
    for i in range(N):
        q = int(order[i]); mode = (3, 1, 2, 3, 3, 1, 1, 2)[i]; o = rng.permutation(8); dg = o[:(FQ, FQ - 1, more, 0, 7, 8, FQ, FQ - 1)[i]]
        full = int(o[0]) if i in (0, 6) else -1; stay = int(o[FQ - 1]) if i in (1, 7) else -1; late = int(o[FQ]) if i == 1 else -1
        hit = i in (0, 2, 4, 5, 6)
        for k in range(8):
            g = int(o[k]); early = bool(np.any(dg == g)); die = early or g == late; cr = np.zeros(V, bool)
            wild = k in (5, 6); part = not (hit or die or wild or g == stay)
            when = 3 if i in (1, 7) and not early and g != stay else mode
            lm[q, g, S - 1], n = pair(rng, die, NU)
            if g == full: lm[q, g, S - 1] = NU - 1; n = NU
            elif g == stay: lm[q, g, S - 1] = 16 if rng.random() < 0.5 else NU; n = NU
            elif k == 7 and not die: n = 0
            du = rng.permutation(NU)[:n]
            for j in range(NU):
                top = 15 if j == 0 else 16
                lm[q, g, NS + j], n = pair(rng, bool(np.any(du == j)), top); ds = 16 - top + rng.permutation(top)[:n]
                for s in range(16 - top, 16):
                    lm[q, g, 16 * j + s], n = pair(rng, bool(np.any(ds == s)), 16)
                    cr[256 * j + 16 * s + rng.permutation(16)[:n]] = True
            if part and k == 7: cr[:] = False
            if wild: a[q, g] = np.where(a[q, g] == 13, 0, a[q, g])
            plant(rng, x[q, g], xb[q, g], a[q, g], cr, when, k == 5, 0 if part or (i == 1 and when == 1) else V // 32)
            if wild:
                x[q, g, :, 13] = LO if hit else HI; xb[q, g, :, 13] = HI; a[q, g, 13] = 15 if hit else 14
            elif g != stay:
                xb[q, g, :, 14 if when == 2 else 15] = LO
            if part and k < 7:
                m = ~cr & (a[q, g] < V); m[14:16] = False
                e = V + GH * rng.integers(0, N - 1, V) + rng.integers(0, 14, V)
                a[q, g] = np.where(m, np.where(rng.random(V) < 0.5, np.arange(V), e), a[q, g])
    return pack(x, xb, a, sg, lm)
def setup_inputs_crowd(rng):
    x, xb, a, sg, lm = parts(rng, 0.06); a = tame(a)
    for q in range(N):
        o = rng.permutation(8)
        for g in range(8):
            k = int(o[g]); cr = np.zeros(V, bool)
            if k in (0, 1): a[q, g] = V - 1
            if k == 4: a[q, g] = W - 1
            if k == 5: a[q, g] = rng.choice(np.array([0, V - 1, V, W - 1, 7]), V)
            if k in (1, 2, 3, 6):
                for j in range(NU):
                    c = int(rng.integers(0, 4)); lm[q, g, 16 * j:16 * j + 16] = (15, 14, 15, 16)[c]
                    if c == 2: lm[q, g, 16 * j + int(rng.integers(0, 16))] = 16
                lm[q, g, NS:NS + NU] = rng.choice(np.array([14, 15, 16]), NU); lm[q, g, S - 1] = (0, NU // 2, NU - 1)[int(rng.integers(0, 3))]
                sg[q, g] = rng.integers(0, 3, S)
            if k == 1:
                cr[V - 2] = True; sg[q, g, NS - 1] = 2; lm[q, g, NS - 1] = 16
            if k in (2, 3, 6): cr[:] = True; cr[14:16] = False
            if k == 3: s = np.arange(1, NS, 2); cr[16 * s + rng.integers(0, 16, len(s))] = False
            if k == 6: cr[int(rng.integers(16, V))] = False
            if k in (1, 2, 3, 6): plant(rng, x[q, g], xb[q, g], a[q, g], cr, 1 if k in (2, 3) else 3, k == 3, 0)
    return pack(x, xb, a, sg, lm)
def setup_inputs_calm(rng):
    x, xb, a, sg, lm = parts(rng, 0.04); a = tame(a)
    late = (5, min(RO - 1, 7))[:RO - 5]; hit = rng.permutation(N)[:len(late)]
    for q in range(N):
        o = rng.permutation(8); used = np.zeros((8, NS), bool)
        for g in range(8):
            k = int(o[g])
            if k == 0: continue
            sup = 1 + rng.permutation(NS - 2)[:NS // 10]; sup[0] = NS - 1; c1 = np.zeros(V, bool); c3 = np.zeros(V, bool)
            used[g, sup] = True
            for j in range(len(sup)):
                s = int(sup[j]); n = 1 + j % 3; w = 16 * s + rng.permutation(16)[:n]
                if k in (1, 4, 6) or (k == 3 and (j >> 1) & 1): c1[w] = True
                else: c3[w] = True
                sg[q, g, s] = 2 if k == 4 else (2, 1, 0, 2, 1)[j % 5]
                if k in (6, 7): lm[q, g, s] = n - 1 + ((j // 3) & 1)
            if k == 6: lm[q, g, NS:NS + NU] = rng.integers(0, 4, NU); sg[q, g, NS:NS + NU] = rng.integers(0, 3, NU)
            if np.any(c1): plant(rng, x[q, g], xb[q, g], a[q, g], c1, 1, k in (4, 6), 0)
            if np.any(c3): plant(rng, x[q, g], xb[q, g], a[q, g], c3, 3, k == 5, 0)
        for i in range(len(late)):
            if int(hit[i]) != q: continue
            for g in range(8):
                if int(o[g]) >= FQ: continue
                s = int(rng.choice(np.flatnonzero(~used[g, GH // 16:]) + GH // 16))
                strike(rng, x[q, g], a[q, g], lm[q, g], s, late[i])
    return pack(x, xb, a, sg, lm)
def check_inputs(d):
    bad = []
    for k, lo, hi in (("x0", 0, 63), ("xi", 0, 63), ("ad", 0, W - 1), ("sg", 0, 2), ("lm", 0, 16)):
        v = np.asarray(d[k]).astype(np.float64)
        if not np.all((v >= lo) & (v <= hi) & (v == np.rint(v))): bad.append("range of " + k)
    return bad
def judge(c, s, m):
    n = np.add.reduce(c.astype(np.int64), axis=-1); die = n > m
    rest = np.add.accumulate(c.astype(np.int64), axis=-1) > 0
    b = np.where((s == 0)[..., None], c, np.where((s == 1)[..., None], rest, (n > 0)[..., None]))
    return b | die[..., None], die
def reference(x0, xi, ad, sg, lm):
    x = x0.astype(np.float32).astype(np.int16).reshape(N, 8, 16, V); xb = xi.astype(np.float32).astype(np.int16).reshape(N, 8, 16, V)
    a0 = np.stack([gentries(e) for e in ad]).astype(np.int64)
    s = sg.astype(np.int64); m = lm.astype(np.int64)
    a = a0; c = np.zeros_like(a0)
    u = np.full_like(a0, -1); w = np.zeros_like(a0)
    inc = np.ones_like(a0)
    for step in range(RO):
        seen = []
        for r in range(N):
            p = [x[r]]
            for d in range(1, N):
                q = (r - d) % N; p.append(x[q][(np.arange(8) + q - r) & 7][:, :, :GH])
            seen.append(np.concatenate(p, axis=2))
        y = np.take_along_axis(np.stack(seen), a[:, :, None, :], 3)
        own = a < V; ao = np.minimum(a, V - 1)
        ia = np.where(own, np.take_along_axis(inc, ao, 2), 0)
        crash = ((c > 0) & (c != ia)) | (np.add.reduce((y < x - DF).astype(np.int64), axis=2) >= TR)
        ua = np.take_along_axis(u, ao, 2); uc = np.take_along_axis(w, ao, 2); got = own & (ua >= 0)
        na = np.where(got, ua, a); nc = np.where(got, uc, c)
        b1, d1 = judge(crash.reshape(N, 8, NS, 16), s[:, :, :NS], m[:, :, :NS])
        b2, d2 = judge(d1.reshape(N, 8, NU, 16), s[:, :, NS:NS + NU], m[:, :, NS:NS + NU])
        b3, d3 = judge(d2.reshape(N, 8, 1, NU), s[:, :, S - 1:], m[:, :, S - 1:])
        rank = np.add.reduce(d3[:, :, 0].astype(np.int64), axis=1) >= FQ
        born = b1 | b2.reshape(N, 8, NS)[..., None] | np.repeat(b3[:, :, 0], 16, axis=2)[..., None] | rank[:, None, None, None]
        born = born.reshape(N, 8, V)
        x = np.where(born[:, :, None], xb, np.maximum(x, y))
        u = np.where(born, -1, a); w = np.where(born, 0, ia)
        a = np.where(born, a0, na); c = np.where(born, 0, nc)
        inc = inc + born
    return {"yx": np.ascontiguousarray(x.reshape(N, 128, V)).astype(np.float32).astype(BF), "ya": np.stack([gtable(e) for e in 16 * a + c]).astype(np.float32),
            "yu": np.stack([gtable(e) for e in np.where(u < 0, -1, 16 * u + w)]).astype(np.float32), "yi": np.stack([gtable(e) for e in inc]).astype(np.float32)}

@@ -1,0 +1,595 @@
+from concourse.bass import DstId, RemoteDMATransfer
+from concourse.mybir import AluOpType, AxisListType, ActivationFunctionType
+
+V, GH, RO, NR = 4096, 128, 6, 8
+WX = V + (NR - 1) * GH
+PITCH = 320
+SCALES = (1.0, 16.0, 256.0, -4096.0, 320.0, -1.0, 64.0, -16.0, 32768.0, 4096.0, -128.0, 3.0 / 128)
+CH = 1024
+ORDER = (2, 0, 3, 1)
+OPT = {
+    "vsel": (1920, 1024, 1024, 1024, 1024, 1664),
+    "relu": ("ssvvvvvv", "ssssvvvv"),
+    "cmp": ("sssv", "vvvv"),
+    "add": ("pppppppp", "ddddpppp"),
+    "piece": 384, "rounds": 40, "shake": 300.0, "seed": 1,
+    "cyc": 1.04, "pe": 0.53, "gat": 1.56, "tt2": 2.0, "fix": 50.0, "wake": 120.0, "dma": 1900.0, "bw": 250.0, "far": 5000.0,
+}
+
+BF, F32, I32, U16 = "bfloat16", "float32", "int32", "uint16"
+SCRATCH = {
+    "xa": ("sbuf", [128, WX], BF), "xb": ("sbuf", [128, WX], BF), "wn": ("sbuf", [128, 3 * V], BF),
+    "gw": ("sbuf", [128, 2 * GH], BF), "offg": ("sbuf", [128, 8], U16), "ch": ("sbuf", [128, 144], BF),
+    "c128": ("sbuf", [128, 128], BF),
+    "dd": ("sbuf", [128, V], BF), "cm": ("sbuf", [128, V], BF), "rl": ("sbuf", [128, V], BF),
+    "mw": ("sbuf", [128, 16 * PITCH], BF), "mg": ("sbuf", [128, V], BF), "ts": ("sbuf", [128, 768], BF),
+    "adi": ("sbuf", [128, 256], I32), "ahi": ("sbuf", [128, 256], I32), "ali": ("sbuf", [128, 256], I32),
+    "sgi": ("sbuf", [128, 276], I32), "lmi": ("sbuf", [128, 276], I32),
+    "e0": ("sbuf", [128, 276], F32), "e1": ("sbuf", [128, 276], F32),
+    "nth": ("sbuf", [128, 280], BF), "nlm": ("sbuf", [128, 280], BF),
+    "offa": ("sbuf", [128, 256], U16), "offm": ("sbuf", [128, 256], U16), "offs": ("sbuf", [128, 256], U16),
+    "a0d": ("sbuf", [128, 512], BF), "adg": ("sbuf", [128, 512], BF), "tn": ("sbuf", [128, 512], BF),
+    "ip": ("sbuf", [128, 256], BF), "ul": ("sbuf", [128, 256], BF), "st": ("sbuf", [128, 256], BF),
+    "cr": ("sbuf", [128, 256], BF), "nb": ("sbuf", [128, 256], BF),
+    "udl": ("sbuf", [128, PITCH], BF), "udh": ("sbuf", [128, PITCH], BF), "inc": ("sbuf", [128, PITCH], BF),
+    "m8": ("sbuf", [128, 256], BF), "mu": ("sbuf", [128, 256], BF), "stab": ("sbuf", [128, 256], BF),
+    "oa": ("sbuf", [128, 256], F32), "ou": ("sbuf", [128, 256], F32), "oi": ("sbuf", [128, 256], F32),
+    "colf": ("sbuf", [128, 144], F32), "colb": ("sbuf", [128, 128], F32), "seli": ("sbuf", [128, 24], F32),
+    "pi": ("sbuf", [128, 4], I32), "pc": ("sbuf", [128, 8], F32), "mk": ("sbuf", [128, 16], F32),
+    "ids": ("sbuf", [128, 128 * len(SCALES)], BF), "bo": ("sbuf", [128, 128], BF), "fm": ("sbuf", [128, 128], BF),
+    "f1": ("sbuf", [128, 128], BF), "f2": ("sbuf", [128, 128], BF), "ones": ("sbuf", [128, 128], BF),
+    "cb": ("sbuf", [128, 144], BF), "bc": ("sbuf", [128, 2048], BF), "sel": ("sbuf", [128, 24], BF),
+    "tbl": ("sbuf", [128, 24], F32), "k1": ("sbuf", [128, 16], BF), "z16": ("sbuf", [128, 16], F32),
+    "d1": ("sbuf", [128, 16], BF), "db": ("sbuf", [128, 32], BF), "us": ("sbuf", [128, 16], BF),
+    "zz": ("sbuf", [128, 16], BF), "n3": ("sbuf", [128, 4], F32), "d3": ("sbuf", [128, 8], BF),
+}
+for _b in range(8):
+    SCRATCH["p%d" % _b] = ("psum", [128, 512], F32)
+SEMAPHORES = (["qv", "qs", "qp", "qg", "snt", "lgh", "lad", "lx", "lx0", "ltb", "lxi", "lmw", "oy", "ol"]
+              + ["arr%d" % t for t in range(RO)] + ["own%d" % k for k in range(4)] + ["acc%d" % k for k in range(8)])
+QSEM = {"v": "qv", "s": "qs", "p": "qp", "g": "qg"}
+ARRANGED = {}
+
+
+def conflicts(ops):
+    hist = {}
+    out = []
+    for n, o in enumerate(ops):
+        deps = set()
+        for acc, wr in ((o["r"], False), (o["w"], True)):
+            for name, lo, hi in acc:
+                ps = SCRATCH[name][0] == "psum"
+                for l2, h2, m, w2 in hist.get(name, ()):
+                    if (ps and (ops[m]["q"] != o["q"] or o["q"] == "p")) or ((wr or w2) and l2 < hi and lo < h2):
+                        deps.add(m)
+        out.append(deps)
+        for acc, wr in ((o["r"], False), (o["w"], True)):
+            for name, lo, hi in acc:
+                h = hist.setdefault(name, [])
+                if wr and SCRATCH[name][0] != "psum":
+                    h[:] = [e for e in h if not (lo <= e[0] and e[1] <= hi)]
+                h.append((lo, hi, n, wr))
+    return out
+
+
+def arrange(ops):
+    pre = conflicts(ops)
+    lastkey = {}
+    for n, o in enumerate(ops):
+        if o["dma"]:
+            if o["key"] in lastkey:
+                pre[n].add(lastkey[o["key"]])
+            lastkey[o["key"]] = n
+        if o["after"] is not None:
+            pre[n].add(o["after"])
+    res = [o["q"] for o in ops]
+    cost = [o["cost"] for o in ops]
+    moved = {}
+    edges = []
+    for n, o in enumerate(ops):
+        if o["bytes"]:
+            moved[n] = len(res)
+            edges.append((n, len(res), 0.7 * OPT["dma"]))
+            res.append("w")
+            cost.append(o["bytes"] / OPT["bw"] + 15.0 * o["inc"])
+    end = len(res)
+    res.append("e")
+    cost.append(0.0)
+    for n, p in enumerate(pre + [set(range(len(ops)))]):
+        to = n if n < len(ops) else end
+        top = {}
+        for m in p:
+            if to != end and ops[n]["after"] == m:
+                edges.append((m, to, OPT["far"] if ops[m]["key"] == "snt" else 0.0))
+                if m in moved and n in moved:
+                    edges.append((moved[m], moved[n], 0.0))
+            elif to != end and ops[m]["dma"] and ops[n]["key"] == ops[m]["key"]:
+                edges.append((m, to, 0.0))
+            elif m in moved:
+                edges.append((moved[m], to, 0.3 * OPT["dma"] + OPT["wake"]))
+            elif ops[m]["dma"] or to == end:
+                edges.append((m, to, ops[m]["lat"]))
+            else:
+                top[m] = 0.0 if ops[m]["q"] == "p" == ops[n]["q"] else ops[m]["lat"] + OPT["wake"]
+        edges += [(m, to, w) for m, w in sorted(top.items())[-40:]]
+    fwd = [[] for _ in res]
+    bwd = [[] for _ in res]
+    for a, b, w in edges:
+        fwd[a].append((b, w))
+        bwd[b].append((a, w))
+
+    def lay(before, after, prio):
+        left = [len(p) for p in before]
+        ready = [0.0] * len(res)
+        start = [0.0] * len(res)
+        used = {}
+        cand = [n for n in range(len(res)) if left[n] == 0]
+        while cand:
+            n = min(cand, key=lambda k: (prio[k], k))
+            cand.remove(n)
+            t = ready[n]
+            busy = used.setdefault(res[n], [])
+            k = len(busy)
+            while k > 0 and busy[k - 1][1] > t:
+                k -= 1
+            while k < len(busy) and busy[k][0] < t + cost[n]:
+                t = max(t, busy[k][1])
+                k += 1
+            busy.insert(k, (t, t + cost[n]))
+            start[n] = t
+            for s, w in after[n]:
+                ready[s] = max(ready[s], t + cost[n] + w)
+                left[s] -= 1
+                if left[s] == 0:
+                    cand.append(s)
+        return start
+    best = lay(bwd, fwd, [float(n) for n in range(len(res))])
+    start = best
+    seed = OPT["seed"]
+    for it in range(OPT["rounds"]):
+        back = lay(fwd, bwd, [-(start[n] + cost[n]) for n in range(len(res))])
+        prio = []
+        for n in range(len(res)):
+            seed = (seed * 1103515245 + 12345) % 2147483648
+            prio.append(-(back[n] + cost[n]) + OPT["shake"] * seed / 2147483648)
+        start = lay(bwd, fwd, prio)
+        if start[end] < best[end]:
+            best = start
+        elif it % 4 == 3:
+            start = best
+    ARRANGED["span"] = best[end]
+    order = []
+    left = [len(p) for p in pre]
+    suc = [[] for _ in ops]
+    for n, p in enumerate(pre):
+        for m in p:
+            suc[m].append(n)
+    cand = [n for n in range(len(ops)) if left[n] == 0]
+    while cand:
+        n = min(cand, key=lambda k: (best[k], k))
+        cand.remove(n)
+        order.append(n)
+        for s in suc[n]:
+            left[s] -= 1
+            if left[s] == 0:
+                cand.append(s)
+    return order
+
+
+def plan(ops):
+    known = {}
+    newest = {}
+    for n, (o, deps) in enumerate(zip(ops, conflicts(ops))):
+        kn = known.setdefault(o["q"], {})
+        best = {}
+        for m in deps:
+            key = ops[m]["key"]
+            if key == "qp" == o["key"]:
+                continue
+            if ops[m]["dma"] and kn.get(key, -1) < m:
+                m = newest[key]
+            if m > best.get(key, -1):
+                best[key] = m
+        waits = []
+        for key, m in sorted(best.items(), key=lambda e: -e[1]):
+            if kn.get(key, -1) >= m:
+                continue
+            waits.append(m)
+            for k2, m2 in ops[m]["clock"].items():
+                if kn.get(k2, -1) < m2:
+                    kn[k2] = m2
+        o["waits"] = waits
+        o["clock"] = dict(kn)
+        o["clock"][o["key"]] = n
+        for m in waits:
+            ops[m]["sig"] = True
+        if o["dma"]:
+            newest[o["key"]] = n
+
+
+def rank_program(g, core, T, topo):
+    rank = T.rank_of(core)
+    if rank is None:
+        return
+    AL, AF = AluOpType, ActivationFunctionType
+    eng = {"v": g.vector, "s": g.scalar, "p": g.tensor, "g": g, "y": g.sync}
+    ops = []
+
+    def ap(x):
+        if not isinstance(x, tuple):
+            return x
+        if isinstance(x[0], tuple):
+            return ap(x[0]).indirect(ap(x[1]))
+        if len(x) == 4:
+            return T[x[0]][:, x[1]:x[2]:x[3]]
+        return T[x[0]][:, x[1]:x[2]]
+
+    def regs(xs):
+        out = []
+        for x in xs:
+            if isinstance(x, tuple):
+                out += regs(x) if isinstance(x[0], tuple) else [x[:3]]
+        return out
+
+    def width(x):
+        return len(range(*x[1:]))
+
+    def put(q, fn, r, w, cost, xw=(), sem=None, inc=0, nbytes=0, lat=0.0, after=None):
+        ops.append({"q": q, "fn": fn, "r": regs(r), "w": regs(w), "xw": list(xw), "dma": sem is not None, "inc": inc,
+                    "key": sem if sem is not None else QSEM[q], "sig": False, "cost": cost, "bytes": nbytes, "lat": lat,
+                    "after": after})
+        return len(ops) - 1
+
+    def took(out, in0, rate=None):
+        if isinstance(in0[0], tuple):
+            rate = OPT["gat"]
+        elif rate is None:
+            rate = 0.5 if SCRATCH[out[0]][2] in (BF, U16) and SCRATCH[in0[0]][2] in (BF, U16) else 1.0
+        return max(64.0, width(out) * rate) * OPT["cyc"] + OPT["fix"]
+
+    def ts(out, in0, s1, s2, op0, op1=None):
+        if op1 is None:
+            put("v", lambda e: e.tensor_scalar(ap(out), ap(in0), ap(s1), None, op0), [in0, s1], [out], took(out, in0))
+        else:
+            put("v", lambda e: e.tensor_scalar(ap(out), ap(in0), ap(s1), ap(s2), op0, op1), [in0, s1, s2], [out], took(out, in0))
+
+    def tt(out, in0, in1, op, xw=(), after=None):
+        rate = 1.0 if not isinstance(in0[0], tuple) and SCRATCH[in0[0]][0] == "psum" else OPT["tt2"]
+        put("v", lambda e: e.tensor_tensor(ap(out), ap(in0), ap(in1), op), [in0, in1], [out], took(out, in0, rate), xw,
+            after=after)
+
+    def cp(out, in_):
+        put("v", lambda e: e.tensor_copy(ap(out), ap(in_)), [in_], [out], took(out, in_))
+
+    def fill(out, c):
+        put("v", lambda e: e.memset(ap(out), c), [], [out], took(out, out))
+
+    def act(out, in_, func, bias=0.0, scale=1.0):
+        put("s", lambda e: e.activation(ap(out), ap(in_), func, bias=bias, scale=ap(scale)), [in_, scale], [out],
+            took(out, in_, 1.0))
+
+    def mms(calls):
+        def fn(e):
+            return [e.matmul(ap(o), ap(lt), ap(rh), a, b) for o, lt, rh, a, b in calls][-1]
+        put("p", fn, [c[1] for c in calls] + [c[2] for c in calls], [c[0] for c in calls],
+            sum(max(64, width(c[2])) for c in calls) * OPT["pe"], lat=60.0)
+
+    def mm(out, terms, start=True, stop=True):
+        mms([(out, lt, rh, start and k == 0, stop and k == len(terms) - 1) for k, (lt, rh) in enumerate(terms)])
+
+    def iota(out, pattern, mult, flag=True):
+        cost = 130.0 + 2 * width(out) * OPT["cyc"]
+        if flag:
+            put("g", lambda e: e.iota(ap(out), pattern, 0, mult, allow_small_or_imprecise_dtypes=True), [], [out], cost)
+        else:
+            put("g", lambda e: e.iota(ap(out), pattern, 0, mult), [], [out], cost)
+
+    def dmas(q, sem, pairs, r, w, nbytes, add=False, after=None):
+        def fn(e):
+            for o, i in pairs:
+                (e.dma_start(o, i, accum_op=AL.add) if add else e.dma_start(o, i)).then_inc(T.sem[sem], 16)
+        return put(q, fn, r, w, 1000.0 if q == "g" else 120.0, (), sem, 16 * len(pairs), nbytes,
+                   OPT["dma"] + nbytes / OPT["bw"], after)
+
+    def turned(sb, hb, step):
+        out = []
+        n = 16 // step
+        for h0, h1, g0 in ((0, NR - rank, rank), (NR - rank, NR, 0)):
+            if h1 > h0:
+                out.append((sb(slice(16 * h0, 16 * h1, step)), hb(slice(n * g0, n * (g0 + h1 - h0)))))
+        return out
+
+    def idm(scale):
+        k = SCALES.index(scale)
+        return ("ids", 128 * k, 128 * k + 128)
+
+    def cn(i, name="cb"):
+        return (name, 15 - i, 143 - i)
+
+    far = [d for d in range(1, NR) if topo.chip(T.cores[(rank + d) % NR]) != topo.chip(core)]
+    near = [d for d in range(1, NR) if d not in far]
+    fmask = topo.mask(core, T.cores[(rank + far[0]) % NR])
+    nmask = topo.mask(core, T.cores[(rank + near[0]) % NR]) & ~fmask
+    nf, nn = bin(fmask).count("1"), bin(nmask).count("1")
+    arrive = nf * len(far) + nn * len(near)
+    sent = {}
+
+    def send(x, t):
+        def dst(d):
+            rid, pid, _ = topo.addr(T.cores[(rank + d) % NR])
+            return DstId(rid=rid, pnc=pid)
+
+        def fn(e):
+            tr = [RemoteDMATransfer(dst_ids=[dst(d) for d in ds], dma_engine_mask=m, remote_sem=T.sem["arr%d" % t],
+                                    srcs=[T[x][:, 0:GH]], dsts=[T[x][:, V + (d - 1) * GH:V + d * GH] for d in ds])
+                  for ds, m in ((far, fmask), (near, nmask))]
+            e.remote_dma_fused(tr, local_sem=T.sem["snt"])
+        sent[t] = put("g", fn, [(x, 0, GH)], [], 500.0, (), "snt", nf + nn, 0, OPT["far"])
+
+    n = dmas("y", "lgh", turned(lambda p: T.xa[p, 0:GH], lambda p: T.x0[p, 0:GH], 1), [], [("xa", 0, GH)], 256 * GH)
+    n = dmas("s", "lad", turned(lambda p: T.adi[p, :], lambda p: T.ad[p, :], 1), [], [("adi", 0, 256)], 512 * 256, after=n)
+    fa, fb = CH * ORDER[0], CH * ORDER[0] + CH
+    n = dmas("y", "lx0", turned(lambda p: T.xa[p, fa:fb], lambda p: T.x0[p, fa:fb], 1), [], [("xa", fa, fb)], 256 * CH, after=n)
+    fill(("sgi", 0, 276), 0)
+    fill(("lmi", 0, 276), 0)
+    dmas("s", "ltb", turned(lambda p: T.sgi[p, 0:273], lambda p: T.sg[p, :], 16)
+         + turned(lambda p: T.lmi[p, 0:273], lambda p: T.lm[p, :], 16), [], [("sgi", 0, 276), ("lmi", 0, 276)], 20000, after=n)
+    n = dmas("y", "lx", turned(lambda p: T.xa[p, GH:fa], lambda p: T.x0[p, GH:fa], 1)
+             + turned(lambda p: T.xa[p, fb:V], lambda p: T.x0[p, fb:V], 1), [], [("xa", GH, fa), ("xa", fb, V)],
+             256 * (V - CH), after=n)
+    for k in ORDER[1:]:
+        a, b = CH * k, CH * k + CH
+        n = dmas("y", "own%d" % k, turned(lambda p: T.wn[p, a:b], lambda p: T.x0[p, a:b], 1), [], [("wn", a, b)], 256 * CH,
+                 after=n)
+    loaded = n
+    iota(("pi", 0, 1), [[0, 1]], 1, False)
+    iota(("colf", 0, 144), [[1, 144]], 0)
+    iota(("colb", 0, 128), [[16, 8], [0, 16]], 0)
+    send("xa", 0)
+    iota(("seli", 0, 24), [[1, 3], [16, 8]], 0)
+    iota(("stab", 0, 256), [[1, 256]], 0)
+    dmas("y", "lxi", turned(lambda p: T.wn[p, V:2 * V], lambda p: T.xi[p, :], 1)
+         + turned(lambda p: T.gw[p, GH:2 * GH], lambda p: T.xi[p, 0:GH], 1), [("xa", GH, fa)],
+         [("wn", V, 2 * V), ("gw", GH, 2 * GH)], 256 * V, after=loaded)
+    P, PB, PM, PO, NF, PG = [("pc", k, k + 1) for k in range(6)]
+    ts(("pi", 1, 2), ("pi", 0, 1), 112, None, AL.bitwise_and)
+    cp(("pc", 0, 2), ("pi", 0, 2))
+    cp(("offa", 0, 256), ("adi", 0, 256))
+    tt(PM, P, PB, AL.subtract)
+    ts(idm(1.0), ("colf", 0, 128), P, None, AL.is_equal)
+    ts(("cb", 0, 144), ("colf", 0, 144), PB, 15.0, AL.subtract, AL.is_equal)
+    ts(("bo", 0, 128), ("colb", 0, 128), PB, None, AL.is_equal)
+    ts(("f1", 0, 128), ("colf", 0, 128), P, 16.0, AL.is_gt, AL.mult)
+    ts(("mk", 0, 16), ("colf", 0, 16), PM, 256.0, AL.is_equal, AL.mult)
+    ts(PO, PM, 4096.0, None, AL.add)
+    ts(PG, PM, float(GH), None, AL.add)
+    ts(("ch", 0, 144), ("cb", 0, 144), 0.5, None, AL.mult)
+    ts(NF, PM, 0.0, -1.0, AL.is_equal, AL.mult)
+    ts(("f2", 0, 128), idm(1.0), 255.0, 1.0, AL.mult, AL.add)
+    for t in range(16):
+        act(("bc", 128 * t, 128 * t + 128), ("bo", 0, 128), AF.Identity, 0.0, ("mk", t, t + 1))
+    for s in SCALES[1:]:
+        act(idm(s), idm(1.0), AF.Identity, 0.0, s)
+    act(("wn", fa, fb), ("xa", fa, fb), AF.Identity)
+    ts(("ahi", 0, 256), ("adi", 0, 256), 4, None, AL.arith_shift_right)
+    ts(("ali", 0, 256), ("adi", 0, 256), 15, None, AL.bitwise_and)
+    ts(("m8", 0, 256), ("adi", 0, 256), float(V), -7.0, AL.is_lt, AL.mult)
+    tt(("f1", 0, 128), ("f1", 0, 128), ("f2", 0, 128), AL.add)
+    ts(("a0d", 256, 512), ("ahi", 0, 256), -128.0, None, AL.add)
+    ts(("a0d", 0, 256), ("ali", 0, 256), 16.0, 8.0, AL.mult, AL.add)
+    ts(("ip", 0, 256), ("ali", 0, 256), 128.0, None, AL.add)
+    tt(("fm", 0, 128), ("f1", 0, 128), ("bo", 0, 128), AL.mult)
+    ts(("e0", 0, 276), ("sgi", 0, 276), 0.0, 240.0, AL.is_equal, AL.mult)
+    ts(("e1", 0, 276), ("sgi", 0, 276), 1.0, 15.0, AL.is_le, AL.mult)
+    ts(("nlm", 0, 276), ("lmi", 0, 276), 1.0, NF, AL.add, AL.mult)
+    tt(("ul", 0, 256), ("a0d", 0, 256), ("m8", 0, 256), AL.add)
+    cp(("adg", 0, 512), ("a0d", 0, 512))
+    tt(("e0", 0, 276), ("e0", 0, 276), ("e1", 0, 276), AL.add)
+    fill(("ones", 0, 128), 1.0)
+    fill(("c128", 0, 128), 128.0)
+    fill(("z16", 0, 16), 0.0)
+    fill(("inc", 0, 256), 1.0)
+    fill(("inc", 256, PITCH), 8.0)
+    fill(("udl", 256, PITCH), 0.0)
+    fill(("udh", 256, PITCH), 0.0)
+    ts(("nth", 0, 276), ("e0", 0, 276), 1.0, NF, AL.add, AL.mult)
+    ts(("sel", 0, 24), ("seli", 0, 24), P, None, AL.is_equal)
+    mm(("p1", 256, 512), [(idm(320.0), ("ip", 0, 256)), (idm(1.0), ("a0d", 256, 512))])
+    mm(("p5", 0, 16), [(cn(t), ("nlm", t, 256, 16)) for t in range(16)])
+    mm(("p5", 16, 17), [(("bo", 0, 128), ("nlm", 272, 273))])
+    mm(("p5", 17, 18), [(("bo", 0, 128), ("nth", 272, 273))])
+    for k in range(16 * PITCH // CH):
+        act(("mw", CH * k, CH * k + CH), ("xa", fa, fb), AF.Identity, 0.0, 0.0)
+    ts(("offm", 0, 256), ("p1", 256, 512), 128.0 - 128.0 * PITCH, None, AL.add)
+    ts(("tbl", 0, 18), ("p5", 0, 18), -1.0, -1.0, AL.mult, AL.add)
+    ts(("k1", 0, 16), ("z16", 0, 16), ("tbl", 17, 18), 15.0, AL.add, AL.is_le)
+    tt(("tbl", 17, 18), ("tbl", 16, 17), ("tbl", 17, 18), AL.min)
+
+    BO, FM, I1 = ("bo", 0, 128), ("fm", 0, 128), idm(1.0)
+    MB = ("p6", "p7", "p0", "p1")
+    for t in range(RO):
+        cur, nxt = ("xa", "xb") if t % 2 == 0 else ("xb", "xa")
+        own, own2 = (0, 2 * V) if t % 2 == 0 else (2 * V, 0)
+        first, last = t == 0, t == RO - 1
+
+        def back(q, h):
+            return (("ts", 384 * h + 128 * q, 384 * h + 128 * q + 128), I1)
+
+        if not first:
+            for h in range(2):
+                for a in (2048 * h, 2048 * h + CH):
+                    act(("mg", a, a + CH), (("mw", 0, 16 * PITCH), ("offm", a // 16, (a + CH) // 16)), AF.Identity)
+                mms([(("p%d" % h, i, 384, 16), ("mg", 2048 * h + i, 2048 * h + 2048, 16), ("sel", 0, 24), True, True)
+                     for i in range(16)])
+                act(("ts", 384 * h, 384 * h + 384), ("p%d" % h, 0, 384), AF.Identity)
+            for h in range(2):
+                a, b = 128 * h, 128 * h + 128
+                mm(("p4", 256 + a, 256 + b), [back(2, h), (idm(16.0), ("ip", a, b)), (idm(-1.0), ("adg", a, b))])
+                mm(("p3", a, b), [back(1, h)])
+            act(("st", 0, 256), ("p4", 256, 512), AF.Relu, -32768.0, 16.0)
+        for k in range(4):
+            a, b = CH * ORDER[k], CH * ORDER[k] + CH
+            tt(("dd", a, b), ((cur, 0, WX), ("offa", a // 16, b // 16)), ("wn", own + a, own + b), AL.subtract,
+               [("arr%d" % t, arrive)] if k == 0 else [], sent[t] if k == 0 else len(ops) - 2)
+            if k > 0:
+                ops[-1]["after"] = None
+                ops[-1]["r"].append(("dd", CH * ORDER[k - 1], CH * ORDER[k - 1] + 1))
+            if OPT["cmp"][0 if first else 1][k] == "s":
+                act(("cm", a, b), ("dd", a, b), AF.Sign, 12.5)
+                mm(("p2", a // 16, b // 16), [(idm(3.0 / 128), ("c128", 0, CH // 16))]
+                   + [(cn(i, "ch"), ("cm", a + i, b, 16)) for i in range(16)])
+            else:
+                ts(("cm", a, b), ("dd", a, b), -12.5, -0.3125, AL.is_gt, AL.add)
+                mm(("p2", a // 16, b // 16), [(cn(i), ("cm", a + i, b, 16)) for i in range(16)])
+        bank = 0
+        for u in range(8):
+            a = CH * ORDER[u // 2] + 512 * (u % 2)
+            b = a + 512
+            if OPT["relu"][0 if first else 1][u] == "v":
+                ts(("rl", a, b), ("dd", a, b), 0.0, None, AL.max)
+            else:
+                act(("rl", a, b), ("dd", a, b), AF.Relu)
+            if OPT["add"][0 if first else 1][u] == "p":
+                pb = MB[bank % 4]
+                bank += 1
+                mm((pb, 0, 512), [(I1, (cur, a, b))], True, False)
+                mm((pb, 0, 512), [(I1, ("rl", a, b))], False, True)
+                if a == 0 and not last:
+                    act(("gw", 0, GH), (pb, 0, GH), AF.Identity)
+                act(("wn", own + a, own + b), (pb, 0, 512), AF.Identity)
+            else:
+                dmas("g", "acc%d" % u, [(T.wn[:, own + a:own + b], T.rl[:, a:b])], [("rl", a, b), ("wn", own + a, own + b)],
+                     [("wn", own + a, own + b)], 512 * 512, True)
+                if a == 0 and not last:
+                    act(("gw", 0, GH), ("wn", own, own + GH), AF.Identity)
+        if not first:
+            ts(("p3", 256, 512), ("p3", 0, 256), 0.0, None, AL.is_equal)
+            tt(("tn", 0, 256), ("p3", 256, 512), ("adg", 0, 256), AL.mult)
+            tt(("tn", 256, 512), ("p3", 256, 512), ("adg", 256, 512), AL.mult)
+            mm(("p3", 0, 512), [(idm(-1.0), ("a0d", 0, 512))], True, False)
+            mms([(("p3", 256 * q + 128 * h, 256 * q + 128 * h + 128),) + back(1 - q, h) + (False, False)
+                 for q in range(2) for h in range(2)])
+            mm(("p3", 0, 512), [(I1, ("tn", 0, 512))], False, True)
+        mm(("p4", 0, 256), [(BO, ("nth", 0, 256))], True, False)
+        if first:
+            ts(("cr", 0, 256), ("p2", 0, 256), 0.0, None, AL.is_le)
+        else:
+            tt(("cr", 0, 256), ("p2", 0, 256), ("st", 0, 256), AL.is_le)
+            for h in range(2):
+                a, b = 128 * h, 128 * h + 128
+                mm(("p2", 256 + a, 256 + b), [back(2, h), (idm(16.0), ("ip", a, b)), (idm(-16.0), ("c128", 0, 128))])
+        mm(("p5", 0, 16), [(cn(k), ("cr", k, 256, 16)) for k in range(16)])
+        mm(("p4", 0, 256), [(FM, ("cr", 0, 256))], False, False)
+        tt(("d1", 0, 16), ("p5", 0, 16), ("tbl", 0, 16), AL.is_gt)
+        mm(("p5", 16, 32), [(BO, ("nlm", 256, 272)), (BO, ("d1", 0, 16))])
+        mm(("p5", 32, 48), [(BO, ("nth", 256, 272)), (FM, ("d1", 0, 16))])
+        ts(("db", 0, 32), ("p5", 16, 48), 0.0, None, AL.is_ge)
+        small = took(("us", 0, 16), ("us", 0, 16))
+        put("v", lambda e: e.tensor_tensor_scan(T.us[:, 0:16], T.k1[:, 0:16], T.db[:, 0:16], 0.0, AL.mult, AL.max),
+            [("k1", 0, 16), ("db", 0, 16)], [("us", 0, 16)], small)
+        put("v", lambda e: e.tensor_reduce(T.n3[:, 0:1], T.db[:, 0:16], AxisListType.X, AL.add),
+            [("db", 0, 16)], [("n3", 0, 1)], small)
+        tt(("zz", 0, 16), ("us", 0, 16), ("db", 16, 32), AL.max)
+        ts(("d3", 0, 2), ("tbl", 16, 18), ("n3", 0, 1), -0.25, AL.is_lt, AL.add)
+        mms([(("p4", k, 256, 16), ("bc", 128 * k, 128 * k + 128), ("zz", 0, 16), False, k == 15) for k in range(16)])
+        mm(("p5", 48, 49), [(("ones", 0, 128), ("d3", 0, 1)), (idm(64.0), ("d3", 1, 2))])
+        ts(("nb", 0, 256), ("p4", 0, 256), ("p5", 48, 49), 0.0, AL.max, AL.is_lt)
+        if not last:
+            mm(("p5", 64, 72), [(idm(16.0), ("stab", 0, 8)), (idm(-128.0), ("nb", 0, 8))])
+            ts(("offg", 0, 8), ("p5", 64, 72), PG, None, AL.add)
+            cp((nxt, 0, GH), (("gw", 0, 2 * GH), ("offg", 0, 8)))
+            send(nxt, t + 1)
+        mm(("p4", 0, 256), [(idm(16.0), ("stab", 0, 256)), (idm(-4096.0 if own == 0 else 4096.0), ("nb", 0, 256))])
+        ts(("offs", 0, 256), ("p4", 0, 256), PO if own == 0 else PM, None, AL.add)
+        mm(("p5", 256, 512), [(I1, ("inc", 0, 256)), (idm(-1.0), ("nb", 0, 256))])
+        mm(("p4", 256, 512), [(I1, ("nb", 0, 256))])
+        act(("oi", 0, 256) if last else ("inc", 0, 256), ("p5", 256, 512), AF.Identity, 1.0)
+        win = ("wn", 0, 2 * V) if own == 0 else ("wn", V, 3 * V)
+        vs = OPT["vsel"][t]
+
+        def pick(q, a, b):
+            if q == "v":
+                cp((nxt, a, b), (win, ("offs", a // 16, b // 16)))
+            else:
+                act((nxt, a, b), (win, ("offs", a // 16, b // 16)), AF.Identity)
+
+        def result(n, y, src, a, b, sem):
+            dmas("y", sem, [(o, i) for i, o in turned(lambda p: T[src][p, a:b], lambda p: y[p, a:b], 1)], [(src, a, b)], [], n)
+
+        if first:
+            tt(("udl", 0, 256), ("p4", 256, 512), ("ul", 0, 256), AL.mult)
+        else:
+            tt(("udl", 0, 256), ("p2", 256, 512), ("nb", 0, 256), AL.mult)
+        tt(("udh", 0, 256), ("p4", 256, 512), ("adg", 256, 512), AL.mult)
+        if not last:
+            dmas("y", "lmw", [(T.mw[q:128:16, :], T[n][:, :]) for q, n in enumerate(("udh", "udl", "inc"))],
+                 [("udh", 0, PITCH), ("udl", 0, PITCH), ("inc", 0, PITCH)], [("mw", 0, 16 * PITCH)], 768 * PITCH)
+        if not first:
+            tt(("p2", 0, 256), ("p3", 0, 256), ("nb", 0, 256), AL.mult)
+            tt(("p2", 256, 512), ("p3", 256, 512), ("nb", 0, 256), AL.mult)
+            tt(("adg", 0, 512), ("p2", 0, 512), ("a0d", 0, 512), AL.add)
+            ts(("ip", 0, 256), ("adg", 0, 256), 0.0625, 127.71875, AL.mult, AL.add)
+        if last:
+            ts(("mu", 0, 256), ("udh", 0, 256), 128.0, -8.0, AL.is_ge, AL.mult)
+            mm(("p3", 0, 256), [(idm(256.0), ("udh", 0, 256)), (I1, ("udl", 0, 256)), (I1, ("mu", 0, 256)),
+                                (idm(32768.0), ("nb", 0, 256)), (I1, ("nb", 0, 256))])
+            ts(("ou", 0, 256), ("p3", 0, 256), -1.0, None, AL.add)
+            mm(("p5", 0, 256), [(I1, ("adg", 0, 256)), (idm(-16.0), ("ip", 0, 256))])
+            ts(("m8", 0, 256), ("p5", 0, 256), -2040.0, -8.0, AL.is_equal, AL.mult)
+            mm(("p4", 0, 256), [(idm(256.0), ("adg", 256, 512)), (I1, ("adg", 0, 256)), (I1, ("m8", 0, 256))])
+            ts(("oa", 0, 256), ("p4", 0, 256), 32768.0, None, AL.add)
+            cut = [vs + (V - vs) * k // 4 // 32 * 32 for k in range(4)] + [V]
+            piece = [vs * k // 3 // 32 * 32 for k in range(3)] + [vs]
+            for k in range(4):
+                pick("s", cut[k], cut[k + 1])
+                if k < 3:
+                    pick("v", piece[k], piece[k + 1])
+            for a, b in (cut[0:2], cut[1:3], piece[0:2], cut[2:4], piece[1:3], cut[3:5], piece[2:4]):
+                result(256 * (b - a), T.yx, nxt, a, b, "oy")
+            for n, y in (("oi", T.yi), ("ou", T.yu), ("oa", T.ya)):
+                result(512 * 256, y, n, 0, 256, "ol")
+        else:
+            if not first:
+                mm(("p5", 256, 512), [(idm(320.0), ("ip", 0, 256)), (I1, ("adg", 256, 512))])
+                mm(("p4", 0, 256), [(idm(16.0), ("adg", 256, 512)), (I1, ("ip", 0, 256))])
+                ts(("offm", 0, 256), ("p5", 256, 512), 128.0 - 128.0 * PITCH, None, AL.add)
+                ts(("offa", 0, 256), ("p4", 0, 256), 1920.0, None, AL.add)
+            pick("s", 2 * CH, 3 * CH)
+            if vs < CH:
+                pick("s", vs, CH)
+            pick("s", max(vs, CH), 2 * CH)
+            pick("s", 3 * CH, V)
+            a = GH
+            while a < vs:
+                b = min(a + OPT["piece"], vs, CH if a < CH else vs)
+                pick("v", a, b)
+                a = b
+            for k in ORDER:
+                a, b = CH * k, CH * k + CH
+                dmas("y", "own%d" % k, [(T.wn[:, own2 + a:own2 + b], T[nxt][:, a:b])], [(nxt, a, b)],
+                     [("wn", own2 + a, own2 + b)], 256 * CH)
+
+    tag = repr(sorted(OPT.items()))
+    if tag not in ARRANGED:
+        ARRANGED[tag] = arrange(ops)
+    ops = [ops[n] for n in ARRANGED[tag]]
+    plan(ops)
+    total = {}
+    for o in ops:
+        if o["dma"]:
+            total[o["key"]] = total.get(o["key"], 0) + o["inc"]
+        elif o["sig"]:
+            total[o["key"]] = total.get(o["key"], 0) + 1
+        o["val"] = total.get(o["key"], 0)
+    for o in ops:
+        e = eng[o["q"]]
+        for m in o["waits"]:
+            e.wait_ge(T.sem[ops[m]["key"]], ops[m]["val"])
+        for s, v in o["xw"]:
+            e.wait_ge(T.sem[s], v)
+        ins = o["fn"](e)
+        if o["sig"] and not o["dma"]:
+            ins.then_inc(T.sem[o["key"]], 1)
+    g.sync.wait_ge(T.sem["oy"], total["oy"])
+    g.sync.wait_ge(T.sem["ol"], total["ol"])
+    g.wait_ge(T.sem["snt"], total["snt"])

@@ -3,52 +3,71 @@ from concourse.mybir import AluOpType, AxisListType, ActivationFunctionType
 
 V, GH, RO, NR = 4096, 128, 6, 8
 WX = V + (NR - 1) * GH
-PITCH = 320
-SCALES = (1.0, 16.0, 256.0, -4096.0, 320.0, -1.0, 64.0, -16.0, 32768.0, 4096.0, -128.0, 3.0 / 128)
+PITCH = 160
+MW = 32 * PITCH
+SW = PITCH + 128
+BIG = 131072.0
+SCALES = (1.0, 16.0, -1024.0, 32.0, float(PITCH), -1.0, 64.0, 8.0, -8.0, 512.0, BIG, 3.0 / 128, -256.0)
 CH = 1024
-ORDER = (2, 0, 3, 1)
 OPT = {
-    "vsel": (1920, 1024, 1024, 1024, 1024, 1664),
-    "relu": ("ssvvvvvv", "ssssvvvv"),
-    "cmp": ("sssv", "vvvv"),
-    "add": ("pppppppp", "ddddpppp"),
-    "piece": 384, "rounds": 40, "shake": 300.0, "seed": 1,
-    "cyc": 1.04, "pe": 0.53, "gat": 1.56, "tt2": 2.0, "fix": 50.0, "wake": 120.0, "dma": 1900.0, "bw": 250.0, "far": 5000.0,
+    "vsel": (2048, 1536, 1536, 1536, 1536, 1792),
+    "relu": ("ssssssvv", "ssssvvss", "ssssvvss"),
+    "cmp": ("sssv", "vvsv", "vvsv"),
+    "add": ("dddd", "dddd", "dddd"),
+    "own": "dddd",
+    "banks": ("36", "74", "01"),
+    "dq": "v", "fast": False, "piece": 512, "cuts": (0, 1024, 2048, 3072, 4096), "crs": False,
+    "first": {
+        "v": "pro kl own kt km g0 g1 g2 g3 c3 late cr ks d1 r6 db r7 sc zz d3 nb offs gp v1 v0 v2 v3",
+        "s": "pro ids bc0 bc1 kl mw2 mw3 late mw4 c0 r1 r0 c1 c2 r3 r2 r5 r4 mw0 uh ul mw1 s0 s1",
+        "p": "km kt pv pu n0 j0 n1 n2 n3 j1 j3 j2 j4 j5 o0 o1",
+        "g": "pro a0 a1 a2 a3 send", "y": "pro wn wi wh wl w0 w2 w1 w3"},
+    "later": {
+        "v": "g0 g1 g2 c0 c1 g3 c3 tv0 cr r4 r5 d1 tv1 db sc zz d3 nb dl offs gp dq dh v0 off v2 v1",
+        "s": "m1 m0 m2 ts0 m3 c2 ts1 r0 r1 st r2 r3 uh r6 r7 ul s0 s1 s2",
+        "p": "T0 sp0 T1 n0 n1 sp1 o0 n2 n3 pu j1 j0 j2 j3 pl j4 j5 pv o1 pa om oa",
+        "g": "a0 a1 a2 a3 send", "y": "wh wn wl wi w0 w1 w2 w3"},
+    "last": {
+        "v": "g7 g0 g1 c0 g2 c1 g3 c3 r5 tv1 tv0 r4 cr d1 db sc d3 zz nb dl offs dq ou v0 f7 dh v1 v2 oa2 v3",
+        "s": "m0 m1 m3 ts0 m2 c2 r0 ts1 r1 r3 st r2 r6 r7 s0 s1 s2 inc s3",
+        "p": "T0 n0 j0 T1 n1 sp0 n2 o0 sp1 n3 po pa j1 j3 pl j2 j5 j4 o1 ou1 f1 pi oa1",
+        "g": "a0 a2 a1 a3", "y": "ou s1 s0 s2 inc v0 oa2 v1 v2 s3 v3"},
 }
 
 BF, F32, I32, U16 = "bfloat16", "float32", "int32", "uint16"
 SCRATCH = {
-    "xa": ("sbuf", [128, WX], BF), "xb": ("sbuf", [128, WX], BF), "wn": ("sbuf", [128, 3 * V], BF),
-    "gw": ("sbuf", [128, 2 * GH], BF), "offg": ("sbuf", [128, 8], U16), "ch": ("sbuf", [128, 144], BF),
-    "c128": ("sbuf", [128, 128], BF),
-    "dd": ("sbuf", [128, V], BF), "cm": ("sbuf", [128, V], BF), "rl": ("sbuf", [128, V], BF),
-    "mw": ("sbuf", [128, 16 * PITCH], BF), "mg": ("sbuf", [128, V], BF), "ts": ("sbuf", [128, 768], BF),
+    "xa": ("sbuf", [128, WX], BF), "xb": ("sbuf", [128, WX], BF), "wn": ("sbuf", [128, 2 * V], BF),
+    "own": ("sbuf", [128, V], BF), "mw": ("sbuf", [128, MW], BF),
+    "dd": ("sbuf", [128, V], BF), "cm": ("sbuf", [128, V], BF), "mg": ("sbuf", [128, V], BF), "ts": ("sbuf", [128, 1024], BF),
+    "ch": ("sbuf", [128, 144], BF), "c128": ("sbuf", [128, 64], BF), "kl": ("sbuf", [128, SW], BF),
     "adi": ("sbuf", [128, 256], I32), "ahi": ("sbuf", [128, 256], I32), "ali": ("sbuf", [128, 256], I32),
     "sgi": ("sbuf", [128, 276], I32), "lmi": ("sbuf", [128, 276], I32),
     "e0": ("sbuf", [128, 276], F32), "e1": ("sbuf", [128, 276], F32),
-    "nth": ("sbuf", [128, 280], BF), "nlm": ("sbuf", [128, 280], BF),
-    "offa": ("sbuf", [128, 256], U16), "offm": ("sbuf", [128, 256], U16), "offs": ("sbuf", [128, 256], U16),
-    "a0d": ("sbuf", [128, 512], BF), "adg": ("sbuf", [128, 512], BF), "tn": ("sbuf", [128, 512], BF),
-    "ip": ("sbuf", [128, 256], BF), "ul": ("sbuf", [128, 256], BF), "st": ("sbuf", [128, 256], BF),
-    "cr": ("sbuf", [128, 256], BF), "nb": ("sbuf", [128, 256], BF),
-    "udl": ("sbuf", [128, PITCH], BF), "udh": ("sbuf", [128, PITCH], BF), "inc": ("sbuf", [128, PITCH], BF),
-    "m8": ("sbuf", [128, 256], BF), "mu": ("sbuf", [128, 256], BF), "stab": ("sbuf", [128, 256], BF),
+    "nth": ("sbuf", [128, 280], BF), "nlm": ("sbuf", [128, 280], BF), "nts": ("sbuf", [128, SW], BF),
+    "off": ("sbuf", [128, 512], U16), "offs": ("sbuf", [128, 256], U16), "offg": ("sbuf", [128, 8], U16),
+    "h0": ("sbuf", [128, 256], BF), "q0": ("sbuf", [128, 256], BF), "ia0": ("sbuf", [128, 256], BF),
+    "hs": ("sbuf", [128, SW], BF), "ls": ("sbuf", [128, SW], BF),
+    "dh": ("sbuf", [128, SW], BF), "dl": ("sbuf", [128, SW], BF), "dq": ("sbuf", [128, SW], BF),
+    "uh": ("sbuf", [128, 2 * PITCH], BF), "ul": ("sbuf", [128, 2 * PITCH], BF), "gr": ("sbuf", [128, 2 * PITCH], BF),
+    "nb": ("sbuf", [128, 2 * PITCH * RO], BF), "nbg": ("sbuf", [128, 8], BF),
+    "st": ("sbuf", [128, 256], BF), "cr": ("sbuf", [128, 256], BF), "g7": ("sbuf", [128, 256], BF), "f7": ("sbuf", [128, 256], BF),
+    "stab": ("sbuf", [128, 256], BF),
     "oa": ("sbuf", [128, 256], F32), "ou": ("sbuf", [128, 256], F32), "oi": ("sbuf", [128, 256], F32),
-    "colf": ("sbuf", [128, 144], F32), "colb": ("sbuf", [128, 128], F32), "seli": ("sbuf", [128, 24], F32),
+    "colf": ("sbuf", [128, 144], F32), "colb": ("sbuf", [128, 128], F32), "seli": ("sbuf", [128, 32], F32),
     "pi": ("sbuf", [128, 4], I32), "pc": ("sbuf", [128, 8], F32), "mk": ("sbuf", [128, 16], F32),
     "ids": ("sbuf", [128, 128 * len(SCALES)], BF), "bo": ("sbuf", [128, 128], BF), "fm": ("sbuf", [128, 128], BF),
     "f1": ("sbuf", [128, 128], BF), "f2": ("sbuf", [128, 128], BF), "ones": ("sbuf", [128, 128], BF),
-    "cb": ("sbuf", [128, 144], BF), "bc": ("sbuf", [128, 2048], BF), "sel": ("sbuf", [128, 24], BF),
-    "tbl": ("sbuf", [128, 24], F32), "k1": ("sbuf", [128, 16], BF), "z16": ("sbuf", [128, 16], F32),
-    "d1": ("sbuf", [128, 16], BF), "db": ("sbuf", [128, 32], BF), "us": ("sbuf", [128, 16], BF),
-    "zz": ("sbuf", [128, 16], BF), "n3": ("sbuf", [128, 4], F32), "d3": ("sbuf", [128, 8], BF),
+    "cb": ("sbuf", [128, 144], BF), "bc": ("sbuf", [128, 2048], BF), "sel": ("sbuf", [128, 32], BF), "se3": ("sbuf", [128, 24], BF),
+    "tbl": ("sbuf", [128, 72], F32), "k1": ("sbuf", [128, 32], BF), "z16": ("sbuf", [128, 16], F32),
+    "d1": ("sbuf", [128, 16], BF), "db": ("sbuf", [128, 48], BF), "us": ("sbuf", [128, 32], F32),
+    "zz": ("sbuf", [128, 16], BF), "d3": ("sbuf", [128, 8], BF),
 }
 for _b in range(8):
     SCRATCH["p%d" % _b] = ("psum", [128, 512], F32)
-SEMAPHORES = (["qv", "qs", "qp", "qg", "snt", "lgh", "lad", "lx", "lx0", "ltb", "lxi", "lmw", "oy", "ol"]
-              + ["arr%d" % t for t in range(RO)] + ["own%d" % k for k in range(4)] + ["acc%d" % k for k in range(8)])
+SEMAPHORES = (["qv", "qs", "qp", "qg", "snt", "lgh", "lad", "lx", "ltb", "lmw", "lmn", "oy", "ol"]
+              + ["arr%d" % t for t in range(RO)] + ["lxi%d" % k for k in range(4)] + ["acc%d" % k for k in range(4)]
+              + ["own%d" % k for k in range(4)])
 QSEM = {"v": "qv", "s": "qs", "p": "qp", "g": "qg"}
-ARRANGED = {}
 
 
 def conflicts(ops):
@@ -60,14 +79,19 @@ def conflicts(ops):
             for name, lo, hi in acc:
                 ps = SCRATCH[name][0] == "psum"
                 for l2, h2, m, w2 in hist.get(name, ()):
+                    if wr and w2 and o["rows"] and ops[m]["rows"] not in (False, o["rows"]):
+                        continue
                     if (ps and (ops[m]["q"] != o["q"] or o["q"] == "p")) or ((wr or w2) and l2 < hi and lo < h2):
                         deps.add(m)
         out.append(deps)
         for acc, wr in ((o["r"], False), (o["w"], True)):
             for name, lo, hi in acc:
                 h = hist.setdefault(name, [])
-                if wr and SCRATCH[name][0] != "psum":
-                    h[:] = [e for e in h if not (lo <= e[0] and e[1] <= hi)]
+                if wr and not o["rows"]:
+                    ps = SCRATCH[name][0] == "psum"
+                    h[:] = [e for e in h if (ps and ops[e[2]]["q"] != o["q"]) or not (lo <= e[0] and e[1] <= hi)]
+                elif wr:
+                    h[:] = [e for e in h if ops[e[2]]["rows"] != o["rows"]]
                 h.append((lo, hi, n, wr))
     return out
 
@@ -75,104 +99,26 @@ def conflicts(ops):
 def arrange(ops):
     pre = conflicts(ops)
     lastkey = {}
-    for n, o in enumerate(ops):
-        if o["dma"]:
-            if o["key"] in lastkey:
-                pre[n].add(lastkey[o["key"]])
-            lastkey[o["key"]] = n
-        if o["after"] is not None:
-            pre[n].add(o["after"])
-    res = [o["q"] for o in ops]
-    cost = [o["cost"] for o in ops]
-    moved = {}
-    edges = []
-    for n, o in enumerate(ops):
-        if o["bytes"]:
-            moved[n] = len(res)
-            edges.append((n, len(res), 0.7 * OPT["dma"]))
-            res.append("w")
-            cost.append(o["bytes"] / OPT["bw"] + 15.0 * o["inc"])
-    end = len(res)
-    res.append("e")
-    cost.append(0.0)
-    for n, p in enumerate(pre + [set(range(len(ops)))]):
-        to = n if n < len(ops) else end
-        top = {}
-        for m in p:
-            if to != end and ops[n]["after"] == m:
-                edges.append((m, to, OPT["far"] if ops[m]["key"] == "snt" else 0.0))
-                if m in moved and n in moved:
-                    edges.append((moved[m], moved[n], 0.0))
-            elif to != end and ops[m]["dma"] and ops[n]["key"] == ops[m]["key"]:
-                edges.append((m, to, 0.0))
-            elif m in moved:
-                edges.append((moved[m], to, 0.3 * OPT["dma"] + OPT["wake"]))
-            elif ops[m]["dma"] or to == end:
-                edges.append((m, to, ops[m]["lat"]))
-            else:
-                top[m] = 0.0 if ops[m]["q"] == "p" == ops[n]["q"] else ops[m]["lat"] + OPT["wake"]
-        edges += [(m, to, w) for m, w in sorted(top.items())[-40:]]
-    fwd = [[] for _ in res]
-    bwd = [[] for _ in res]
-    for a, b, w in edges:
-        fwd[a].append((b, w))
-        bwd[b].append((a, w))
-
-    def lay(before, after, prio):
-        left = [len(p) for p in before]
-        ready = [0.0] * len(res)
-        start = [0.0] * len(res)
-        used = {}
-        cand = [n for n in range(len(res)) if left[n] == 0]
-        while cand:
-            n = min(cand, key=lambda k: (prio[k], k))
-            cand.remove(n)
-            t = ready[n]
-            busy = used.setdefault(res[n], [])
-            k = len(busy)
-            while k > 0 and busy[k - 1][1] > t:
-                k -= 1
-            while k < len(busy) and busy[k][0] < t + cost[n]:
-                t = max(t, busy[k][1])
-                k += 1
-            busy.insert(k, (t, t + cost[n]))
-            start[n] = t
-            for s, w in after[n]:
-                ready[s] = max(ready[s], t + cost[n] + w)
-                left[s] -= 1
-                if left[s] == 0:
-                    cand.append(s)
-        return start
-    best = lay(bwd, fwd, [float(n) for n in range(len(res))])
-    start = best
-    seed = OPT["seed"]
-    for it in range(OPT["rounds"]):
-        back = lay(fwd, bwd, [-(start[n] + cost[n]) for n in range(len(res))])
-        prio = []
-        for n in range(len(res)):
-            seed = (seed * 1103515245 + 12345) % 2147483648
-            prio.append(-(back[n] + cost[n]) + OPT["shake"] * seed / 2147483648)
-        start = lay(bwd, fwd, prio)
-        if start[end] < best[end]:
-            best = start
-        elif it % 4 == 3:
-            start = best
-    ARRANGED["span"] = best[end]
-    order = []
-    left = [len(p) for p in pre]
     suc = [[] for _ in ops]
+    for n, o in enumerate(ops):
+        lastkey[o["key"]] = n
+        if o["xw"]:
+            pre[n].add(lastkey["snt"])
+    for q in "vspgy":
+        line = sorted((o["place"], n) for n, o in enumerate(ops) if o["q"] == q)
+        for (_, m), (_, n) in zip(line, line[1:]):
+            pre[n].add(m)
     for n, p in enumerate(pre):
         for m in p:
             suc[m].append(n)
-    cand = [n for n in range(len(ops)) if left[n] == 0]
-    while cand:
-        n = min(cand, key=lambda k: (best[k], k))
-        cand.remove(n)
-        order.append(n)
+    left = [len(p) for p in pre]
+    order = [n for n in range(len(ops)) if left[n] == 0]
+    for n in order:
         for s in suc[n]:
             left[s] -= 1
             if left[s] == 0:
-                cand.append(s)
+                order.append(s)
+    assert len(order) == len(ops)
     return order
 
 
@@ -214,6 +160,10 @@ def rank_program(g, core, T, topo):
     AL, AF = AluOpType, ActivationFunctionType
     eng = {"v": g.vector, "s": g.scalar, "p": g.tensor, "g": g, "y": g.sync}
     ops = []
+    now = [0, "pro"]
+
+    def at(name):
+        now[1] = name
 
     def ap(x):
         if not isinstance(x, tuple):
@@ -231,65 +181,52 @@ def rank_program(g, core, T, topo):
                 out += regs(x) if isinstance(x[0], tuple) else [x[:3]]
         return out
 
-    def width(x):
-        return len(range(*x[1:]))
-
-    def put(q, fn, r, w, cost, xw=(), sem=None, inc=0, nbytes=0, lat=0.0, after=None):
+    def put(q, fn, r, w, xw=(), sem=None, inc=0, rows=False):
+        names = OPT["first" if now[0] == 0 else "last" if now[0] == RO - 1 else "later"][q].split()
         ops.append({"q": q, "fn": fn, "r": regs(r), "w": regs(w), "xw": list(xw), "dma": sem is not None, "inc": inc,
-                    "key": sem if sem is not None else QSEM[q], "sig": False, "cost": cost, "bytes": nbytes, "lat": lat,
-                    "after": after})
-        return len(ops) - 1
-
-    def took(out, in0, rate=None):
-        if isinstance(in0[0], tuple):
-            rate = OPT["gat"]
-        elif rate is None:
-            rate = 0.5 if SCRATCH[out[0]][2] in (BF, U16) and SCRATCH[in0[0]][2] in (BF, U16) else 1.0
-        return max(64.0, width(out) * rate) * OPT["cyc"] + OPT["fix"]
+                    "key": sem if sem is not None else QSEM[q], "sig": False, "rows": rows,
+                    "place": (now[0], names.index(now[1]))})
 
     def ts(out, in0, s1, s2, op0, op1=None):
         if op1 is None:
-            put("v", lambda e: e.tensor_scalar(ap(out), ap(in0), ap(s1), None, op0), [in0, s1], [out], took(out, in0))
+            put("v", lambda e: e.tensor_scalar(ap(out), ap(in0), ap(s1), None, op0), [in0, s1], [out])
         else:
-            put("v", lambda e: e.tensor_scalar(ap(out), ap(in0), ap(s1), ap(s2), op0, op1), [in0, s1, s2], [out], took(out, in0))
+            put("v", lambda e: e.tensor_scalar(ap(out), ap(in0), ap(s1), ap(s2), op0, op1), [in0, s1, s2], [out])
 
-    def tt(out, in0, in1, op, xw=(), after=None):
-        rate = 1.0 if not isinstance(in0[0], tuple) and SCRATCH[in0[0]][0] == "psum" else OPT["tt2"]
-        put("v", lambda e: e.tensor_tensor(ap(out), ap(in0), ap(in1), op), [in0, in1], [out], took(out, in0, rate), xw,
-            after=after)
+    def tt(out, in0, in1, op, xw=()):
+        put("v", lambda e: e.tensor_tensor(ap(out), ap(in0), ap(in1), op), [in0, in1], [out], xw)
 
     def cp(out, in_):
-        put("v", lambda e: e.tensor_copy(ap(out), ap(in_)), [in_], [out], took(out, in_))
+        put("v", lambda e: e.tensor_copy(ap(out), ap(in_)), [in_], [out])
 
     def fill(out, c):
-        put("v", lambda e: e.memset(ap(out), c), [], [out], took(out, out))
+        put("v", lambda e: e.memset(ap(out), c), [], [out])
 
     def act(out, in_, func, bias=0.0, scale=1.0):
-        put("s", lambda e: e.activation(ap(out), ap(in_), func, bias=bias, scale=ap(scale)), [in_, scale], [out],
-            took(out, in_, 1.0))
+        put("s", lambda e: e.activation(ap(out), ap(in_), func, bias=bias, scale=ap(scale)), [in_, scale], [out])
 
     def mms(calls):
         def fn(e):
             return [e.matmul(ap(o), ap(lt), ap(rh), a, b) for o, lt, rh, a, b in calls][-1]
-        put("p", fn, [c[1] for c in calls] + [c[2] for c in calls], [c[0] for c in calls],
-            sum(max(64, width(c[2])) for c in calls) * OPT["pe"], lat=60.0)
+        put("p", fn, [c[1] for c in calls] + [c[2] for c in calls], [c[0] for c in calls])
+
+    def grp(terms, start=True, stop=True):
+        mms([c + (start and k == 0, stop and k == len(terms) - 1) for k, c in enumerate(terms)])
 
     def mm(out, terms, start=True, stop=True):
-        mms([(out, lt, rh, start and k == 0, stop and k == len(terms) - 1) for k, (lt, rh) in enumerate(terms)])
+        grp([(out, lt, rh) for lt, rh in terms], start, stop)
 
     def iota(out, pattern, mult, flag=True):
-        cost = 130.0 + 2 * width(out) * OPT["cyc"]
         if flag:
-            put("g", lambda e: e.iota(ap(out), pattern, 0, mult, allow_small_or_imprecise_dtypes=True), [], [out], cost)
+            put("g", lambda e: e.iota(ap(out), pattern, 0, mult, allow_small_or_imprecise_dtypes=True), [], [out])
         else:
-            put("g", lambda e: e.iota(ap(out), pattern, 0, mult), [], [out], cost)
+            put("g", lambda e: e.iota(ap(out), pattern, 0, mult), [], [out])
 
-    def dmas(q, sem, pairs, r, w, nbytes, add=False, after=None):
+    def dmas(q, sem, pairs, r, w, add=False, rows=False):
         def fn(e):
             for o, i in pairs:
                 (e.dma_start(o, i, accum_op=AL.add) if add else e.dma_start(o, i)).then_inc(T.sem[sem], 16)
-        return put(q, fn, r, w, 1000.0 if q == "g" else 120.0, (), sem, 16 * len(pairs), nbytes,
-                   OPT["dma"] + nbytes / OPT["bw"], after)
+        put(q, fn, r, w, (), sem, 16 * len(pairs), rows)
 
     def turned(sb, hb, step):
         out = []
@@ -306,13 +243,32 @@ def rank_program(g, core, T, topo):
     def cn(i, name="cb"):
         return (name, 15 - i, 143 - i)
 
+    def join(bank, col, scale, name, h=None, base=0):
+        a, n = (0, 128) if h is None else (64 * h, 64)
+        return [((bank, col + 2 * a + p, col + 2 * a + 2 * n, 2), idm(scale),
+                 (name, base + PITCH * p + a, base + PITCH * p + a + n)) for p in range(2)]
+
+    def split(bank, scale, name):
+        lt = idm(scale) if isinstance(scale, float) else scale
+        return [((bank, PITCH * p, PITCH * p + 128), lt, (name, p, 256, 2)) for p in range(2)]
+
+    def whole(bank, scale, name):
+        return [((bank, 0, SW), idm(scale), (name, 0, SW))]
+
+    def back(bank, q, h, col=0):
+        return [((bank, col + 128 * h, col + 128 * h + 128), ("ts", 512 * h + 128 * q, 512 * h + 128 * q + 128), idm(1.0))]
+
+    def backs(bank, q, scale=1.0):
+        _, a, b = idm(scale)
+        return [((bank, PITCH * p + 64 * h, PITCH * p + 64 * h + 64), ("ts", 512 * h + 128 * q, 512 * h + 128 * q + 128),
+                 ("ids", a + p, b, 2)) for h in range(2) for p in range(2)]
+
     far = [d for d in range(1, NR) if topo.chip(T.cores[(rank + d) % NR]) != topo.chip(core)]
     near = [d for d in range(1, NR) if d not in far]
     fmask = topo.mask(core, T.cores[(rank + far[0]) % NR])
     nmask = topo.mask(core, T.cores[(rank + near[0]) % NR]) & ~fmask
     nf, nn = bin(fmask).count("1"), bin(nmask).count("1")
     arrive = nf * len(far) + nn * len(near)
-    sent = {}
 
     def send(x, t):
         def dst(d):
@@ -324,255 +280,361 @@ def rank_program(g, core, T, topo):
                                     srcs=[T[x][:, 0:GH]], dsts=[T[x][:, V + (d - 1) * GH:V + d * GH] for d in ds])
                   for ds, m in ((far, fmask), (near, nmask))]
             e.remote_dma_fused(tr, local_sem=T.sem["snt"])
-        sent[t] = put("g", fn, [(x, 0, GH)], [], 500.0, (), "snt", nf + nn, 0, OPT["far"])
+        put("g", fn, [(x, 0, GH)], [], (), "snt", nf + nn)
 
-    n = dmas("y", "lgh", turned(lambda p: T.xa[p, 0:GH], lambda p: T.x0[p, 0:GH], 1), [], [("xa", 0, GH)], 256 * GH)
-    n = dmas("s", "lad", turned(lambda p: T.adi[p, :], lambda p: T.ad[p, :], 1), [], [("adi", 0, 256)], 512 * 256, after=n)
-    fa, fb = CH * ORDER[0], CH * ORDER[0] + CH
-    n = dmas("y", "lx0", turned(lambda p: T.xa[p, fa:fb], lambda p: T.x0[p, fa:fb], 1), [], [("xa", fa, fb)], 256 * CH, after=n)
+    def spread(q, name, sem, base=0):
+        dmas("y", sem, [(T.mw[q:128:16, 16 * PITCH * p:16 * PITCH * (p + 1)],
+                         T[name][:, base + PITCH * p:base + PITCH * (p + 1)]) for p in range(2)],
+             [(name, base, base + 2 * PITCH)], [("mw", 0, MW)], rows=q + 1)
+
+    dmas("y", "lgh", turned(lambda p: T.xa[p, 0:GH], lambda p: T.x0[p, 0:GH], 1), [], [("xa", 0, GH)])
+    dmas("s", "lad", turned(lambda p: T.adi[p, :], lambda p: T.ad[p, :], 1), [], [("adi", 0, 256)])
     fill(("sgi", 0, 276), 0)
     fill(("lmi", 0, 276), 0)
+    dmas("y", "lx", turned(lambda p: T.xa[p, GH:V], lambda p: T.x0[p, GH:V], 1), [], [("xa", GH, V)])
     dmas("s", "ltb", turned(lambda p: T.sgi[p, 0:273], lambda p: T.sg[p, :], 16)
-         + turned(lambda p: T.lmi[p, 0:273], lambda p: T.lm[p, :], 16), [], [("sgi", 0, 276), ("lmi", 0, 276)], 20000, after=n)
-    n = dmas("y", "lx", turned(lambda p: T.xa[p, GH:fa], lambda p: T.x0[p, GH:fa], 1)
-             + turned(lambda p: T.xa[p, fb:V], lambda p: T.x0[p, fb:V], 1), [], [("xa", GH, fa), ("xa", fb, V)],
-             256 * (V - CH), after=n)
-    for k in ORDER[1:]:
-        a, b = CH * k, CH * k + CH
-        n = dmas("y", "own%d" % k, turned(lambda p: T.wn[p, a:b], lambda p: T.x0[p, a:b], 1), [], [("wn", a, b)], 256 * CH,
-                 after=n)
-    loaded = n
+         + turned(lambda p: T.lmi[p, 0:273], lambda p: T.lm[p, :], 16), [], [("sgi", 0, 276), ("lmi", 0, 276)])
     iota(("pi", 0, 1), [[0, 1]], 1, False)
     iota(("colf", 0, 144), [[1, 144]], 0)
     iota(("colb", 0, 128), [[16, 8], [0, 16]], 0)
     send("xa", 0)
-    iota(("seli", 0, 24), [[1, 3], [16, 8]], 0)
-    iota(("stab", 0, 256), [[1, 256]], 0)
-    dmas("y", "lxi", turned(lambda p: T.wn[p, V:2 * V], lambda p: T.xi[p, :], 1)
-         + turned(lambda p: T.gw[p, GH:2 * GH], lambda p: T.xi[p, 0:GH], 1), [("xa", GH, fa)],
-         [("wn", V, 2 * V), ("gw", GH, 2 * GH)], 256 * V, after=loaded)
-    P, PB, PM, PO, NF, PG = [("pc", k, k + 1) for k in range(6)]
+    for k in range(1, 4):
+        dmas("y", "own%d" % k, turned(lambda p: T.own[p, CH * k:CH * k + CH], lambda p: T.x0[p, CH * k:CH * k + CH], 1),
+             [("xa", GH, V)], [("own", CH * k, CH * k + CH)])
+    for k in range(4):
+        a = 2 * CH * k + CH
+        dmas("y", "lxi%d" % k, turned(lambda p: T.wn[p, a:a + CH], lambda p: T.xi[p, CH * k:CH * k + CH], 1),
+             [], [("wn", a, a + CH)])
+    iota(("seli", 0, 32), [[1, 4], [16, 8]], 0)
+    iota(("stab", 0, 256), [[0, 4], [1, 64]], 0)
+    P, PB, PM, PO, NF, L0, L1 = [("pc", k, k + 1) for k in range(7)]
+    BO, FM, I1 = ("bo", 0, 128), ("fm", 0, 128), idm(1.0)
     ts(("pi", 1, 2), ("pi", 0, 1), 112, None, AL.bitwise_and)
     cp(("pc", 0, 2), ("pi", 0, 2))
-    cp(("offa", 0, 256), ("adi", 0, 256))
     tt(PM, P, PB, AL.subtract)
     ts(idm(1.0), ("colf", 0, 128), P, None, AL.is_equal)
     ts(("cb", 0, 144), ("colf", 0, 144), PB, 15.0, AL.subtract, AL.is_equal)
-    ts(("bo", 0, 128), ("colb", 0, 128), PB, None, AL.is_equal)
+    ts(BO, ("colb", 0, 128), PB, None, AL.is_equal)
     ts(("f1", 0, 128), ("colf", 0, 128), P, 16.0, AL.is_gt, AL.mult)
     ts(("mk", 0, 16), ("colf", 0, 16), PM, 256.0, AL.is_equal, AL.mult)
-    ts(PO, PM, 4096.0, None, AL.add)
-    ts(PG, PM, float(GH), None, AL.add)
+    ts(PO, PM, float(CH), None, AL.add)
     ts(("ch", 0, 144), ("cb", 0, 144), 0.5, None, AL.mult)
     ts(NF, PM, 0.0, -1.0, AL.is_equal, AL.mult)
+    ts(L0, PM, -8.0, -1.0, AL.mult, AL.add)
+    ts(L1, PM, -8.0, -129.0, AL.mult, AL.add)
     ts(("f2", 0, 128), idm(1.0), 255.0, 1.0, AL.mult, AL.add)
-    for t in range(16):
-        act(("bc", 128 * t, 128 * t + 128), ("bo", 0, 128), AF.Identity, 0.0, ("mk", t, t + 1))
+    fill(("ones", 0, 128), 1.0)
+    fill(("c128", 0, 64), 128.0)
+    fill(("z16", 0, 16), 0.0)
+    tt(("f1", 0, 128), ("f1", 0, 128), ("f2", 0, 128), AL.add)
+    cp(("off", 0, 256), ("adi", 0, 256))
+    tt(FM, ("f1", 0, 128), BO, AL.mult)
+    ts(("ahi", 0, 256), ("adi", 0, 256), 5, None, AL.arith_shift_right)
+    ts(("ali", 0, 256), ("adi", 0, 256), 31, None, AL.bitwise_and)
+    ts(("ia0", 0, 256), ("off", 0, 256), float(V), -6.0, AL.is_lt, AL.mult)
+    ts(("q0", 0, 256), ("ali", 0, 256), -192.0, None, AL.add)
+    cp(("h0", 0, 256), ("ahi", 0, 256))
+    at("ids")
     for s in SCALES[1:]:
         act(idm(s), idm(1.0), AF.Identity, 0.0, s)
-    act(("wn", fa, fb), ("xa", fa, fb), AF.Identity)
-    ts(("ahi", 0, 256), ("adi", 0, 256), 4, None, AL.arith_shift_right)
-    ts(("ali", 0, 256), ("adi", 0, 256), 15, None, AL.bitwise_and)
-    ts(("m8", 0, 256), ("adi", 0, 256), float(V), -7.0, AL.is_lt, AL.mult)
-    tt(("f1", 0, 128), ("f1", 0, 128), ("f2", 0, 128), AL.add)
-    ts(("a0d", 256, 512), ("ahi", 0, 256), -128.0, None, AL.add)
-    ts(("a0d", 0, 256), ("ali", 0, 256), 16.0, 8.0, AL.mult, AL.add)
-    ts(("ip", 0, 256), ("ali", 0, 256), 128.0, None, AL.add)
-    tt(("fm", 0, 128), ("f1", 0, 128), ("bo", 0, 128), AL.mult)
-    ts(("e0", 0, 276), ("sgi", 0, 276), 0.0, 240.0, AL.is_equal, AL.mult)
-    ts(("e1", 0, 276), ("sgi", 0, 276), 1.0, 15.0, AL.is_le, AL.mult)
+    for t in range(16):
+        at("bc%d" % (t // 8))
+        act(("bc", 128 * t, 128 * t + 128), BO, AF.Identity, 0.0, ("mk", t, t + 1))
+    at("kl")
+    fill(("kl", 0, SW), -1536.0)
+    fill(("dh", 0, SW), 0.0)
+    fill(("dl", 0, SW), 0.0)
+    fill(("dq", 0, SW), 192.0)
+    fill(("gr", 0, 2 * PITCH), -5.0)
+    fill(("nb", 0, 2 * PITCH * RO), 1.0)
+    fill(("k1", 16, 17), 0.0)
+    fill(("k1", 17, 32), 1.0)
+    for name, c in (("hs", 0.0), ("ls", -1536.0), ("nts", 0.0)):
+        fill((name, 128, PITCH), c)
+    fill(("uh", SW, 2 * PITCH), 0.0)
+    fill(("ul", SW, 2 * PITCH), 0.0)
+    for p, own in enumerate((L0, L1)):
+        a, b = PITCH * p, PITCH * p + 128
+        fill(("gr", a, b), 1.0)
+        act(("hs", a, b), ("colf", 0, 128), AF.Identity, 0.0, -1.0)
+        act(("ls", a, b), ("ones", 0, 128), AF.Identity, 0.0, own)
+    at("ks")
+    ts(("sel", 0, 32), ("seli", 0, 32), P, None, AL.is_equal)
+    ts(("se3", 0, 8), ("sel", 24, 32), -512.0, None, AL.mult)
+    ts(("se3", 8, 16), ("sel", 24, 32), -512.0, None, AL.mult)
+    ts(("se3", 16, 24), ("seli", 16, 24), P, None, AL.is_le)
+    ts(("sel", 16, 24), ("seli", 16, 24), 5.0, P, AL.add, AL.is_ge)
+    tt(("sel", 0, 16), ("sel", 0, 16), ("se3", 0, 16), AL.add)
+    tt(("sel", 16, 24), ("sel", 16, 24), ("se3", 16, 24), AL.mult)
+    at("km")
+    mm(("p1", 0, 256), [(idm(float(PITCH)), ("q0", 0, 256)), (I1, ("h0", 0, 256))])
+    ts(("off", 256, 512), ("p1", 0, 256), 192.0 * PITCH, None, AL.add)
+    at("kt")
+    ts(("e0", 0, 276), ("sgi", 0, 276), -239.5, 256.0, AL.mult, AL.add)
     ts(("nlm", 0, 276), ("lmi", 0, 276), 1.0, NF, AL.add, AL.mult)
-    tt(("ul", 0, 256), ("a0d", 0, 256), ("m8", 0, 256), AL.add)
-    cp(("adg", 0, 512), ("a0d", 0, 512))
-    tt(("e0", 0, 276), ("e0", 0, 276), ("e1", 0, 276), AL.add)
-    fill(("ones", 0, 128), 1.0)
-    fill(("c128", 0, 128), 128.0)
-    fill(("z16", 0, 16), 0.0)
-    fill(("inc", 0, 256), 1.0)
-    fill(("inc", 256, PITCH), 8.0)
-    fill(("udl", 256, PITCH), 0.0)
-    fill(("udh", 256, PITCH), 0.0)
-    ts(("nth", 0, 276), ("e0", 0, 276), 1.0, NF, AL.add, AL.mult)
-    ts(("sel", 0, 24), ("seli", 0, 24), P, None, AL.is_equal)
-    mm(("p1", 256, 512), [(idm(320.0), ("ip", 0, 256)), (idm(1.0), ("a0d", 256, 512))])
+    ts(("nth", 0, 276), ("e0", 0, 276), 1.0, NF, AL.max, AL.mult)
     mm(("p5", 0, 16), [(cn(t), ("nlm", t, 256, 16)) for t in range(16)])
-    mm(("p5", 16, 17), [(("bo", 0, 128), ("nlm", 272, 273))])
-    mm(("p5", 17, 18), [(("bo", 0, 128), ("nth", 272, 273))])
-    for k in range(16 * PITCH // CH):
-        act(("mw", CH * k, CH * k + CH), ("xa", fa, fb), AF.Identity, 0.0, 0.0)
-    ts(("offm", 0, 256), ("p1", 256, 512), 128.0 - 128.0 * PITCH, None, AL.add)
+    mm(("p5", 16, 17), [(BO, ("nlm", 272, 273))])
+    mm(("p5", 17, 18), [(BO, ("nth", 272, 273))])
+    mms([(("p5", a, a + 16), BO, (name, 256, 272), True, True) for a, name in ((24, "nlm"), (40, "nlm"), (56, "nth"))])
+    for k in range(MW // CH):
+        at("mw%d" % k)
+        act(("mw", CH * k, CH * k + CH), ("ids", 0, CH), AF.Identity, 1.0, 0.0)
+    at("own")
+    cp(("own", 0, CH), ("xa", 0, CH))
+    at("late")
+    for p in range(2):
+        act(("nts", PITCH * p, PITCH * p + 128), ("nth", p, 256, 2), AF.Identity)
     ts(("tbl", 0, 18), ("p5", 0, 18), -1.0, -1.0, AL.mult, AL.add)
-    ts(("k1", 0, 16), ("z16", 0, 16), ("tbl", 17, 18), 15.0, AL.add, AL.is_le)
+    ts(("tbl", 24, 72), ("p5", 24, 72), -1.0, None, AL.mult)
+    ts(("k1", 0, 16), ("z16", 0, 16), ("tbl", 17, 18), 16.0, AL.add, AL.is_le)
     tt(("tbl", 17, 18), ("tbl", 16, 17), ("tbl", 17, 18), AL.min)
 
-    BO, FM, I1 = ("bo", 0, 128), ("fm", 0, 128), idm(1.0)
-    MB = ("p6", "p7", "p0", "p1")
     for t in range(RO):
         cur, nxt = ("xa", "xb") if t % 2 == 0 else ("xb", "xa")
-        own, own2 = (0, 2 * V) if t % 2 == 0 else (2 * V, 0)
         first, last = t == 0, t == RO - 1
-
-        def back(q, h):
-            return (("ts", 384 * h + 128 * q, 384 * h + 128 * q + 128), I1)
+        o = 0 if first else 2 if last else 1
+        now[0] = t
+        nb = 2 * PITCH * t
+        NB = ("nb", nb, nb + SW)
 
         if not first:
             for h in range(2):
-                for a in (2048 * h, 2048 * h + CH):
-                    act(("mg", a, a + CH), (("mw", 0, 16 * PITCH), ("offm", a // 16, (a + CH) // 16)), AF.Identity)
-                mms([(("p%d" % h, i, 384, 16), ("mg", 2048 * h + i, 2048 * h + 2048, 16), ("sel", 0, 24), True, True)
+                for k in (2 * h, 2 * h + 1):
+                    at("m%d" % k)
+                    act(("mg", CH * k, CH * k + CH), (("mw", 0, MW), ("off", 256 + 64 * k, 320 + 64 * k)), AF.Identity)
+                at("T%d" % h)
+                mms([(("p%d" % h, i, 512, 16), ("mg", 2048 * h + i, 2048 * h + 2048, 16), ("sel", 0, 32), True, True)
                      for i in range(16)])
-                act(("ts", 384 * h, 384 * h + 384), ("p%d" % h, 0, 384), AF.Identity)
+                at("ts%d" % h)
+                act(("ts", 512 * h + 256, 512 * h + 512), ("p%d" % h, 256, 512), AF.Identity, 1.0, -1.0)
+                at("tv%d" % h)
+                ts(("ts", 512 * h, 512 * h + 256), ("p%d" % h, 0, 256), 512.0, 256.0, AL.add, AL.min)
             for h in range(2):
-                a, b = 128 * h, 128 * h + 128
-                mm(("p4", 256 + a, 256 + b), [back(2, h), (idm(16.0), ("ip", a, b)), (idm(-1.0), ("adg", a, b))])
-                mm(("p3", a, b), [back(1, h)])
-            act(("st", 0, 256), ("p4", 256, 512), AF.Relu, -32768.0, 16.0)
-        for k in range(4):
-            a, b = CH * ORDER[k], CH * ORDER[k] + CH
-            tt(("dd", a, b), ((cur, 0, WX), ("offa", a // 16, b // 16)), ("wn", own + a, own + b), AL.subtract,
-               [("arr%d" % t, arrive)] if k == 0 else [], sent[t] if k == 0 else len(ops) - 2)
+                at("sp%d" % h)
+                grp(back("p3", 2, h) + join("p3", 0, -1.0, "dl", h) + join("p3", 0, 8.0, "dq", h))
+            at("st")
+            act(("st", 0, 256), ("p3", 0, 256), AF.Relu, -16.0 * 1537, 16.0)
+        cuts = OPT["cuts"]
+        for k, (a, b) in enumerate(zip(cuts, cuts[1:])):
+            at("g%d" % k)
+            tt(("dd", a, b), ((cur, 0, WX), ("off", a // 16, b // 16)), ("own", a, b), AL.subtract,
+               [("arr%d" % t, arrive)] if k == 0 else [])
             if k > 0:
-                ops[-1]["after"] = None
-                ops[-1]["r"].append(("dd", CH * ORDER[k - 1], CH * ORDER[k - 1] + 1))
-            if OPT["cmp"][0 if first else 1][k] == "s":
+                ops[-1]["r"].append(("dd", 0, 1))
+            at("c%d" % k)
+            if (OPT["cmp"][o] + "v")[k] == "s":
                 act(("cm", a, b), ("dd", a, b), AF.Sign, 12.5)
-                mm(("p2", a // 16, b // 16), [(idm(3.0 / 128), ("c128", 0, CH // 16))]
+                at("n%d" % k)
+                mm(("p2", a // 16, b // 16), [(idm(3.0 / 128), ("c128", 0, (b - a) // 16))]
                    + [(cn(i, "ch"), ("cm", a + i, b, 16)) for i in range(16)])
             else:
                 ts(("cm", a, b), ("dd", a, b), -12.5, -0.3125, AL.is_gt, AL.add)
+                at("n%d" % k)
                 mm(("p2", a // 16, b // 16), [(cn(i), ("cm", a + i, b, 16)) for i in range(16)])
+        if not last:
+            at("wi")
+            if first:
+                spread(2, "gr", "lmw")
+            else:
+                spread(3 + t, "nb", "lmw", nb - 2 * PITCH)
+            at("pu")
+            grp(whole("p0", 1.0, "hs") + whole("p0", 1.0, "dh") + split("p0", 1.0, "h0"))
+            at("pv")
+            grp(whole("p1", 1.0, "ls") + whole("p1", 8.0, "dq") + split("p1", 8.0, "q0")
+                + (split("p1", 1.0, "ia0") + [(("p1", PITCH * p, PITCH * p + 128), I1, ("ones", 0, 128)) for p in range(2)]
+                   if first else backs("p1", 2)))
+            for q, (name, bank) in enumerate((("uh", "p0"), ("ul", "p1"))):
+                at(name)
+                act((name, 0, SW), (bank, 0, SW), AF.Identity)
+                at("w" + name[1])
+                spread(q, name, "lmw")
+        banks = ["p" + c for c in OPT["banks"][o]]
         bank = 0
-        for u in range(8):
-            a = CH * ORDER[u // 2] + 512 * (u % 2)
-            b = a + 512
-            if OPT["relu"][0 if first else 1][u] == "v":
-                ts(("rl", a, b), ("dd", a, b), 0.0, None, AL.max)
-            else:
-                act(("rl", a, b), ("dd", a, b), AF.Relu)
-            if OPT["add"][0 if first else 1][u] == "p":
-                pb = MB[bank % 4]
-                bank += 1
-                mm((pb, 0, 512), [(I1, (cur, a, b))], True, False)
-                mm((pb, 0, 512), [(I1, ("rl", a, b))], False, True)
-                if a == 0 and not last:
-                    act(("gw", 0, GH), (pb, 0, GH), AF.Identity)
-                act(("wn", own + a, own + b), (pb, 0, 512), AF.Identity)
-            else:
-                dmas("g", "acc%d" % u, [(T.wn[:, own + a:own + b], T.rl[:, a:b])], [("rl", a, b), ("wn", own + a, own + b)],
-                     [("wn", own + a, own + b)], 512 * 512, True)
-                if a == 0 and not last:
-                    act(("gw", 0, GH), ("wn", own, own + GH), AF.Identity)
+        for k in range(4):
+            for u in (2 * k, 2 * k + 1):
+                a = 512 * u
+                m = ("wn", a + CH * k, a + CH * k + 512)
+                at("r%d" % u)
+                if OPT["add"][o][k] == "q":
+                    pb = (banks[bank % len(banks)], 0, 512)
+                    bank += 1
+                    at("x%d" % u)
+                    mm(pb, [(I1, (cur, a, a + 512))], True, False)
+                    at("y%d" % u)
+                    mm(pb, [(I1, ("dd", a, a + 512))], False, True)
+                    at("e%d" % u)
+                    tt(m, pb, ("own", a, a + 512), AL.max)
+                elif OPT["relu"][o][u] == "v":
+                    ts(m, ("dd", a, a + 512), 0.0, None, AL.max)
+                else:
+                    act(m, ("dd", a, a + 512), AF.Relu)
+                if OPT["add"][o][k] == "p":
+                    pb = (banks[bank % len(banks)], 0, 512)
+                    bank += 1
+                    at("x%d" % u)
+                    mm(pb, [(I1, (cur, a, a + 512))], True, False)
+                    at("y%d" % u)
+                    mm(pb, [(I1, m)], False, True)
+                    at("e%d" % u)
+                    act(m, pb, AF.Identity)
+            if OPT["add"][o][k] == "d":
+                a, m = CH * k, ("wn", 2 * CH * k, 2 * CH * k + CH)
+                at("a%d" % k)
+                dmas("g", "acc%d" % k, [(ap(m), ap((cur, a, a + CH)))], [(cur, a, a + CH), m], [m], True)
         if not first:
-            ts(("p3", 256, 512), ("p3", 0, 256), 0.0, None, AL.is_equal)
-            tt(("tn", 0, 256), ("p3", 256, 512), ("adg", 0, 256), AL.mult)
-            tt(("tn", 256, 512), ("p3", 256, 512), ("adg", 256, 512), AL.mult)
-            mm(("p3", 0, 512), [(idm(-1.0), ("a0d", 0, 512))], True, False)
-            mms([(("p3", 256 * q + 128 * h, 256 * q + 128 * h + 128),) + back(1 - q, h) + (False, False)
-                 for q in range(2) for h in range(2)])
-            mm(("p3", 0, 512), [(I1, ("tn", 0, 512))], False, True)
-        mm(("p4", 0, 256), [(BO, ("nth", 0, 256))], True, False)
-        if first:
-            ts(("cr", 0, 256), ("p2", 0, 256), 0.0, None, AL.is_le)
-        else:
-            tt(("cr", 0, 256), ("p2", 0, 256), ("st", 0, 256), AL.is_le)
-            for h in range(2):
-                a, b = 128 * h, 128 * h + 128
-                mm(("p2", 256 + a, 256 + b), [back(2, h), (idm(16.0), ("ip", a, b)), (idm(-16.0), ("c128", 0, 128))])
-        mm(("p5", 0, 16), [(cn(k), ("cr", k, 256, 16)) for k in range(16)])
-        mm(("p4", 0, 256), [(FM, ("cr", 0, 256))], False, False)
-        tt(("d1", 0, 16), ("p5", 0, 16), ("tbl", 0, 16), AL.is_gt)
-        mm(("p5", 16, 32), [(BO, ("nlm", 256, 272)), (BO, ("d1", 0, 16))])
-        mm(("p5", 32, 48), [(BO, ("nth", 256, 272)), (FM, ("d1", 0, 16))])
-        ts(("db", 0, 32), ("p5", 16, 48), 0.0, None, AL.is_ge)
-        small = took(("us", 0, 16), ("us", 0, 16))
-        put("v", lambda e: e.tensor_tensor_scan(T.us[:, 0:16], T.k1[:, 0:16], T.db[:, 0:16], 0.0, AL.mult, AL.max),
-            [("k1", 0, 16), ("db", 0, 16)], [("us", 0, 16)], small)
-        put("v", lambda e: e.tensor_reduce(T.n3[:, 0:1], T.db[:, 0:16], AxisListType.X, AL.add),
-            [("db", 0, 16)], [("n3", 0, 1)], small)
-        tt(("zz", 0, 16), ("us", 0, 16), ("db", 16, 32), AL.max)
-        ts(("d3", 0, 2), ("tbl", 16, 18), ("n3", 0, 1), -0.25, AL.is_lt, AL.add)
-        mms([(("p4", k, 256, 16), ("bc", 128 * k, 128 * k + 128), ("zz", 0, 16), False, k == 15) for k in range(16)])
-        mm(("p5", 48, 49), [(("ones", 0, 128), ("d3", 0, 1)), (idm(64.0), ("d3", 1, 2))])
-        ts(("nb", 0, 256), ("p4", 0, 256), ("p5", 48, 49), 0.0, AL.max, AL.is_lt)
-        if not last:
-            mm(("p5", 64, 72), [(idm(16.0), ("stab", 0, 8)), (idm(-128.0), ("nb", 0, 8))])
-            ts(("offg", 0, 8), ("p5", 64, 72), PG, None, AL.add)
-            cp((nxt, 0, GH), (("gw", 0, 2 * GH), ("offg", 0, 8)))
-            send(nxt, t + 1)
-        mm(("p4", 0, 256), [(idm(16.0), ("stab", 0, 256)), (idm(-4096.0 if own == 0 else 4096.0), ("nb", 0, 256))])
-        ts(("offs", 0, 256), ("p4", 0, 256), PO if own == 0 else PM, None, AL.add)
-        mm(("p5", 256, 512), [(I1, ("inc", 0, 256)), (idm(-1.0), ("nb", 0, 256))])
-        mm(("p4", 256, 512), [(I1, ("nb", 0, 256))])
-        act(("oi", 0, 256) if last else ("inc", 0, 256), ("p5", 256, 512), AF.Identity, 1.0)
-        win = ("wn", 0, 2 * V) if own == 0 else ("wn", V, 3 * V)
-        vs = OPT["vsel"][t]
-
-        def pick(q, a, b):
-            if q == "v":
-                cp((nxt, a, b), (win, ("offs", a // 16, b // 16)))
-            else:
-                act((nxt, a, b), (win, ("offs", a // 16, b // 16)), AF.Identity)
-
-        def result(n, y, src, a, b, sem):
-            dmas("y", sem, [(o, i) for i, o in turned(lambda p: T[src][p, a:b], lambda p: y[p, a:b], 1)], [(src, a, b)], [], n)
-
-        if first:
-            tt(("udl", 0, 256), ("p4", 256, 512), ("ul", 0, 256), AL.mult)
-        else:
-            tt(("udl", 0, 256), ("p2", 256, 512), ("nb", 0, 256), AL.mult)
-        tt(("udh", 0, 256), ("p4", 256, 512), ("adg", 256, 512), AL.mult)
-        if not last:
-            dmas("y", "lmw", [(T.mw[q:128:16, :], T[n][:, :]) for q, n in enumerate(("udh", "udl", "inc"))],
-                 [("udh", 0, PITCH), ("udl", 0, PITCH), ("inc", 0, PITCH)], [("mw", 0, 16 * PITCH)], 768 * PITCH)
-        if not first:
-            tt(("p2", 0, 256), ("p3", 0, 256), ("nb", 0, 256), AL.mult)
-            tt(("p2", 256, 512), ("p3", 256, 512), ("nb", 0, 256), AL.mult)
-            tt(("adg", 0, 512), ("p2", 0, 512), ("a0d", 0, 512), AL.add)
-            ts(("ip", 0, 256), ("adg", 0, 256), 0.0625, 127.71875, AL.mult, AL.add)
+            at("pa")
+            grp(whole("p3", 1.0, "dh") + backs("p3", 0) + backs("p3", 3, -256.0))
+            at("pl")
+            grp(whole("p6", 8.0, "dq") + whole("p6", 1.0, "kl") + backs("p6", 1) + backs("p6", 3, -256.0))
         if last:
-            ts(("mu", 0, 256), ("udh", 0, 256), 128.0, -8.0, AL.is_ge, AL.mult)
-            mm(("p3", 0, 256), [(idm(256.0), ("udh", 0, 256)), (I1, ("udl", 0, 256)), (I1, ("mu", 0, 256)),
-                                (idm(32768.0), ("nb", 0, 256)), (I1, ("nb", 0, 256))])
-            ts(("ou", 0, 256), ("p3", 0, 256), -1.0, None, AL.add)
-            mm(("p5", 0, 256), [(I1, ("adg", 0, 256)), (idm(-16.0), ("ip", 0, 256))])
-            ts(("m8", 0, 256), ("p5", 0, 256), -2040.0, -8.0, AL.is_equal, AL.mult)
-            mm(("p4", 0, 256), [(idm(256.0), ("adg", 256, 512)), (I1, ("adg", 0, 256)), (I1, ("m8", 0, 256))])
-            ts(("oa", 0, 256), ("p4", 0, 256), 32768.0, None, AL.add)
-            cut = [vs + (V - vs) * k // 4 // 32 * 32 for k in range(4)] + [V]
-            piece = [vs * k // 3 // 32 * 32 for k in range(3)] + [vs]
-            for k in range(4):
-                pick("s", cut[k], cut[k + 1])
-                if k < 3:
-                    pick("v", piece[k], piece[k + 1])
-            for a, b in (cut[0:2], cut[1:3], piece[0:2], cut[2:4], piece[1:3], cut[3:5], piece[2:4]):
-                result(256 * (b - a), T.yx, nxt, a, b, "oy")
-            for n, y in (("oi", T.yi), ("ou", T.yu), ("oa", T.ya)):
-                result(512 * 256, y, n, 0, 256, "ol")
-        else:
-            if not first:
-                mm(("p5", 256, 512), [(idm(320.0), ("ip", 0, 256)), (I1, ("adg", 256, 512))])
-                mm(("p4", 0, 256), [(idm(16.0), ("adg", 256, 512)), (I1, ("ip", 0, 256))])
-                ts(("offm", 0, 256), ("p5", 256, 512), 128.0 - 128.0 * PITCH, None, AL.add)
-                ts(("offa", 0, 256), ("p4", 0, 256), 1920.0, None, AL.add)
-            pick("s", 2 * CH, 3 * CH)
-            if vs < CH:
-                pick("s", vs, CH)
-            pick("s", max(vs, CH), 2 * CH)
-            pick("s", 3 * CH, V)
-            a = GH
-            while a < vs:
-                b = min(a + OPT["piece"], vs, CH if a < CH else vs)
-                pick("v", a, b)
-                a = b
-            for k in ORDER:
-                a, b = CH * k, CH * k + CH
-                dmas("y", "own%d" % k, [(T.wn[:, own2 + a:own2 + b], T[nxt][:, a:b])], [(nxt, a, b)],
-                     [("wn", own2 + a, own2 + b)], 256 * CH)
+            at("g7")
+            ts(("g7", 0, 256), ("off", 0, 256), float(V), -7.0, AL.is_ge, AL.mult)
+            at("po")
+            grp([(("p2", 256, 512), idm(512.0), ("h0", 0, 256)), (("p2", 256, 512), idm(16.0), ("q0", 0, 256)),
+                 (("p2", 256, 512), I1, ("g7", 0, 256))] + join("p2", 256, 512.0, "dh") + join("p2", 256, 16.0, "dq")
+                + back("p2", 2, 0, 256) + back("p2", 2, 1, 256), True, False)
+        fast = OPT["fast"] and not last
+        at("j0")
+        mm(("p4", 0, SW), [(BO, ("nts", 0, SW))], True, False)
+        at("o0")
+        mm(("p7", 0, 256), [(idm(16.0), ("stab", 0, 256))], True, False)
+        c = cuts[-2] // 16 if OPT["crs"] else 0
+        for name, a, b in (("cq", 0, c), ("cr", c, 256)):
+            at(name)
+            if a == b:
+                continue
+            if first:
+                ts(("cr", a, b), ("p2", a, b), 0.0, None, AL.is_le)
+            else:
+                tt(("cr", a, b), ("p2", a, b), ("st", a, b), AL.is_le)
+        at("j1")
+        mm(("p5", 0, 16), [(cn(k), ("cr", k, 256, 16)) for k in range(16)])
+        at("j2")
+        grp(split("p4", FM, "cr"), False, False)
+        if fast:
+            at("h0")
+            mm(("p2", 256, 264), [(BO, ("nth", 0, 8)), (FM, ("cr", 0, 8))], True, False)
+        at("d1")
+        tt(("d1", 0, 16), ("p5", 0, 16), ("tbl", 0, 16), AL.is_gt)
+        at("j3")
+        mms([(("p5", a, a + 16), lt, ("d1", 0, 16), True, True) for a, lt in ((16, BO), (32, BO), (48, FM))])
+        at("db")
+        tt(("db", 0, 48), ("p5", 16, 64), ("tbl", 24, 72), AL.is_ge)
+        at("sc")
+        put("v", lambda e: e.tensor_tensor_scan(T.us[:, 0:32], T.k1[:, 0:32], T.db[:, 0:32], 0.0, AL.mult, AL.add),
+            [("k1", 0, 32), ("db", 0, 32)], [("us", 0, 32)])
+        at("zz")
+        tt(("zz", 0, 16), ("us", 0, 16), ("db", 32, 48), AL.max)
+        at("d3")
+        ts(("d3", 0, 2), ("tbl", 16, 18), ("us", 31, 32), -0.25, AL.is_lt, AL.add)
+        if fast:
+            at("h1")
+            grp([(("p2", 256 + k, 257 + k), ("bc", 128 * k, 128 * k + 128), ("zz", 0, 1)) for k in range(8)], False, True)
+        at("j4")
+        grp([(("p4", PITCH * (k % 2) + k // 2, PITCH * (k % 2) + 128, 8), ("bc", 128 * k, 128 * k + 128), ("zz", 0, 16))
+             for k in range(16)], False, True)
+        at("j5")
+        mm(("p5", 64, 65), [(("ones", 0, 128), ("d3", 0, 1)), (idm(64.0), ("d3", 1, 2))])
+        if fast:
+            at("nbg")
+            ts(("nbg", 0, 8), ("p2", 256, 264), ("p5", 64, 65), 0.0, AL.max, AL.is_lt)
+            at("h2")
+            mm(("p2", 272, 280), [(idm(16.0), ("stab", 0, 8)), (idm(-1024.0), ("nbg", 0, 8))])
+            at("offg")
+            ts(("offg", 0, 8), ("p2", 272, 280), PO, None, AL.add)
+        at("nb")
+        for a in (0, PITCH):
+            ts(("nb", nb + a, nb + a + 128), ("p4", a, a + 128), ("p5", 64, 65), 0.0, AL.max, AL.is_lt)
+        at("o1")
+        grp(join("p7", 0, -1024.0, "nb", None, nb), False, True)
+        at("offs")
+        ts(("offs", 0, 256), ("p7", 0, 256), PO, None, AL.add)
 
-    tag = repr(sorted(OPT.items()))
-    if tag not in ARRANGED:
-        ARRANGED[tag] = arrange(ops)
-    ops = [ops[n] for n in ARRANGED[tag]]
+        def pick(q, a, b, off="offs"):
+            k = a // CH
+            src = (("wn", 2 * CH * k, 2 * CH * k + 2 * CH), (off, a // 16, b // 16))
+            if q == "v":
+                cp((nxt, a, b), src)
+            else:
+                act((nxt, a, b), src, AF.Identity)
+
+        def result(y, src, a, b, sem):
+            dmas("y", sem, [(o, i) for i, o in turned(lambda p: T[src][p, a:b], lambda p: y[p, a:b], 1)], [(src, a, b)], [])
+
+        if not last:
+            at("gp")
+            pick("v", 0, GH, "offg" if fast else "offs")
+            at("send")
+            send(nxt, t + 1)
+            at("wn")
+            spread(3, "nb", "lmn", nb)
+        else:
+            at("pi")
+            for p in range(2):
+                grp([join("p4", 0, -1.0, "nb", None, 2 * PITCH * k)[p] for k in range(RO)])
+            at("inc")
+            act(("oi", 0, 256), ("p4", 0, 256), AF.Identity, RO + 1.0)
+            result(T.yi, "oi", 0, 256, "ol")
+            at("ou1")
+            grp(join("p2", 256, BIG, "nb", None, nb), False, True)
+            at("ou")
+            ts(("ou", 0, 256), ("p2", 256, 512), 6.0 - BIG, -1.0, AL.add, AL.max)
+            result(T.yu, "ou", 0, 256, "ol")
+        if not first:
+            at("dl")
+            tt(("dl", 0, SW), ("p6", 0, SW), NB, AL.mult)
+            at("dh")
+            tt(("dh", 0, SW), ("p3", 0, SW), NB, AL.mult)
+            at("dq")
+            if OPT["dq"] == "v":
+                ts(("dq", 0, SW), ("dl", 0, SW), 0.125, 192.375, AL.mult, AL.add)
+            else:
+                act(("dq", 0, SW), ("dl", 0, SW), AF.Identity, 192.375, 0.125)
+        if last:
+            at("f1")
+            for p in range(2):
+                grp([join("p1", 0, 1.0, "dl")[p], join("p1", 0, -8.0, "dq")[p]])
+            at("f7")
+            ts(("f7", 0, 256), ("p1", 0, 256), -1536.0, -7.0, AL.is_equal, AL.mult)
+            at("oa1")
+            grp([(("p2", 0, 256), idm(512.0), ("h0", 0, 256)), (("p2", 0, 256), idm(16.0), ("q0", 0, 256))]
+                + join("p2", 0, 512.0, "dh") + join("p2", 0, 8.0, "dq") + join("p2", 0, 1.0, "dl")
+                + [(("p2", 0, 256), I1, ("f7", 0, 256))])
+            at("oa2")
+            ts(("oa", 0, 256), ("p2", 0, 256), 1543.0, None, AL.add)
+            result(T.ya, "oa", 0, 256, "ol")
+        elif not first:
+            at("om")
+            grp([(("p2", 256, 512), I1, ("h0", 0, 256)), (("p2", 256, 512), idm(float(PITCH)), ("q0", 0, 256))]
+                + join("p2", 256, 1.0, "dh") + join("p2", 256, float(PITCH), "dq"))
+            at("oa")
+            grp([(("p2", 0, 256), idm(32.0), ("h0", 0, 256)), (("p2", 0, 256), I1, ("q0", 0, 256))]
+                + join("p2", 0, 32.0, "dh") + join("p2", 0, 1.0, "dq"))
+            at("off")
+            cp(("off", 0, 512), ("p2", 0, 512))
+        vs = OPT["vsel"][t]
+        for q, a, end, most in (("s", 0 if last else GH, V - vs, 768 if last else CH), ("v", V - vs, V, OPT["piece"])):
+            n = 0
+            while a < end:
+                b = min((a // most + 1) * most if q == "v" else a + most, end, (a // CH + 1) * CH)
+                at(q + str(min(n, 3 if q == "v" or last else 2)))
+                pick(q, a, b)
+                if last:
+                    result(T.yx, nxt, a, b, "oy")
+                a = b
+                n += 1
+        for k in range(0 if last else 4):
+            a, b = CH * k, CH * k + CH
+            at("w%d" % k)
+            if OPT["own"][k] == "v":
+                cp(("own", a, b), (nxt, a, b))
+            elif OPT["own"][k] == "s":
+                act(("own", a, b), (nxt, a, b), AF.Identity)
+            else:
+                dmas("y", "own%d" % k, [(T.own[:, a:b], T[nxt][:, a:b])], [(nxt, a, b)], [("own", a, b)])
+
+    ops = [ops[n] for n in arrange(ops)]
     plan(ops)
     total = {}
     for o in ops:

from concourse.bass import DstId, RemoteDMATransfer
from concourse.mybir import AluOpType, AxisListType, ActivationFunctionType

V, GH, RO, NR = 4096, 128, 6, 8
WX = V + (NR - 1) * GH
PITCH = 160
MW = 32 * PITCH
SW = PITCH + 128
BIG = 131072.0
SCALES = (1.0, 16.0, -1024.0, 32.0, float(PITCH), -1.0, 64.0, 8.0, -8.0, 512.0, BIG, 3.0 / 128, -256.0)
CH = 1024
OPT = {
    "vsel": (2048, 1536, 1536, 1536, 1536, 1792),
    "relu": ("ssssssvv", "ssssvvss", "ssssvvss"),
    "cmp": ("sssv", "vvsv", "vvsv"),
    "add": ("dddd", "dddd", "dddd"),
    "own": "dddd",
    "banks": ("36", "74", "01"),
    "dq": "v", "fast": False, "piece": 512, "cuts": (0, 1024, 2048, 3072, 4096), "crs": False,
    "first": {
        "v": "pro kl own kt km g0 g1 g2 g3 c3 late cr ks d1 r6 db r7 sc zz d3 nb offs gp v1 v0 v2 v3",
        "s": "pro ids bc0 bc1 kl mw2 mw3 late mw4 c0 r1 r0 c1 c2 r3 r2 r5 r4 mw0 uh ul mw1 s0 s1",
        "p": "km kt pv pu n0 j0 n1 n2 n3 j1 j3 j2 j4 j5 o0 o1",
        "g": "pro a0 a1 a2 a3 send", "y": "pro wn wi wh wl w0 w2 w1 w3"},
    "later": {
        "v": "g0 g1 g2 c0 c1 g3 c3 tv0 cr r4 r5 d1 tv1 db sc zz d3 nb dl offs gp dq dh v0 off v2 v1",
        "s": "m1 m0 m2 ts0 m3 c2 ts1 r0 r1 st r2 r3 uh r6 r7 ul s0 s1 s2",
        "p": "T0 sp0 T1 n0 n1 sp1 o0 n2 n3 pu j1 j0 j2 j3 pl j4 j5 pv o1 pa om oa",
        "g": "a0 a1 a2 a3 send", "y": "wh wn wl wi w0 w1 w2 w3"},
    "last": {
        "v": "g7 g0 g1 c0 g2 c1 g3 c3 r5 tv1 tv0 r4 cr d1 db sc d3 zz nb dl offs dq ou v0 f7 dh v1 v2 oa2 v3",
        "s": "m0 m1 m3 ts0 m2 c2 r0 ts1 r1 r3 st r2 r6 r7 s0 s1 s2 inc s3",
        "p": "T0 n0 j0 T1 n1 sp0 n2 o0 sp1 n3 po pa j1 j3 pl j2 j5 j4 o1 ou1 f1 pi oa1",
        "g": "a0 a2 a1 a3", "y": "ou s1 s0 s2 inc v0 oa2 v1 v2 s3 v3"},
}

BF, F32, I32, U16 = "bfloat16", "float32", "int32", "uint16"
SCRATCH = {
    "xa": ("sbuf", [128, WX], BF), "xb": ("sbuf", [128, WX], BF), "wn": ("sbuf", [128, 2 * V], BF),
    "own": ("sbuf", [128, V], BF), "mw": ("sbuf", [128, MW], BF),
    "dd": ("sbuf", [128, V], BF), "cm": ("sbuf", [128, V], BF), "mg": ("sbuf", [128, V], BF), "ts": ("sbuf", [128, 1024], BF),
    "ch": ("sbuf", [128, 144], BF), "c128": ("sbuf", [128, 64], BF), "kl": ("sbuf", [128, SW], BF),
    "adi": ("sbuf", [128, 256], I32), "ahi": ("sbuf", [128, 256], I32), "ali": ("sbuf", [128, 256], I32),
    "sgi": ("sbuf", [128, 276], I32), "lmi": ("sbuf", [128, 276], I32),
    "e0": ("sbuf", [128, 276], F32), "e1": ("sbuf", [128, 276], F32),
    "nth": ("sbuf", [128, 280], BF), "nlm": ("sbuf", [128, 280], BF), "nts": ("sbuf", [128, SW], BF),
    "off": ("sbuf", [128, 512], U16), "offs": ("sbuf", [128, 256], U16), "offg": ("sbuf", [128, 8], U16),
    "h0": ("sbuf", [128, 256], BF), "q0": ("sbuf", [128, 256], BF), "ia0": ("sbuf", [128, 256], BF),
    "hs": ("sbuf", [128, SW], BF), "ls": ("sbuf", [128, SW], BF),
    "dh": ("sbuf", [128, SW], BF), "dl": ("sbuf", [128, SW], BF), "dq": ("sbuf", [128, SW], BF),
    "uh": ("sbuf", [128, 2 * PITCH], BF), "ul": ("sbuf", [128, 2 * PITCH], BF), "gr": ("sbuf", [128, 2 * PITCH], BF),
    "nb": ("sbuf", [128, 2 * PITCH * RO], BF), "nbg": ("sbuf", [128, 8], BF),
    "st": ("sbuf", [128, 256], BF), "cr": ("sbuf", [128, 256], BF), "g7": ("sbuf", [128, 256], BF), "f7": ("sbuf", [128, 256], BF),
    "stab": ("sbuf", [128, 256], BF),
    "oa": ("sbuf", [128, 256], F32), "ou": ("sbuf", [128, 256], F32), "oi": ("sbuf", [128, 256], F32),
    "colf": ("sbuf", [128, 144], F32), "colb": ("sbuf", [128, 128], F32), "seli": ("sbuf", [128, 32], F32),
    "pi": ("sbuf", [128, 4], I32), "pc": ("sbuf", [128, 8], F32), "mk": ("sbuf", [128, 16], F32),
    "ids": ("sbuf", [128, 128 * len(SCALES)], BF), "bo": ("sbuf", [128, 128], BF), "fm": ("sbuf", [128, 128], BF),
    "f1": ("sbuf", [128, 128], BF), "f2": ("sbuf", [128, 128], BF), "ones": ("sbuf", [128, 128], BF),
    "cb": ("sbuf", [128, 144], BF), "bc": ("sbuf", [128, 2048], BF), "sel": ("sbuf", [128, 32], BF), "se3": ("sbuf", [128, 24], BF),
    "tbl": ("sbuf", [128, 72], F32), "k1": ("sbuf", [128, 32], BF), "z16": ("sbuf", [128, 16], F32),
    "d1": ("sbuf", [128, 16], BF), "db": ("sbuf", [128, 48], BF), "us": ("sbuf", [128, 32], F32),
    "zz": ("sbuf", [128, 16], BF), "d3": ("sbuf", [128, 8], BF),
}
for _b in range(8):
    SCRATCH["p%d" % _b] = ("psum", [128, 512], F32)
SEMAPHORES = (["qv", "qs", "qp", "qg", "snt", "lgh", "lad", "lx", "ltb", "lmw", "lmn", "oy", "ol"]
              + ["arr%d" % t for t in range(RO)] + ["lxi%d" % k for k in range(4)] + ["acc%d" % k for k in range(4)]
              + ["own%d" % k for k in range(4)])
QSEM = {"v": "qv", "s": "qs", "p": "qp", "g": "qg"}


def conflicts(ops):
    hist = {}
    out = []
    for n, o in enumerate(ops):
        deps = set()
        for acc, wr in ((o["r"], False), (o["w"], True)):
            for name, lo, hi in acc:
                ps = SCRATCH[name][0] == "psum"
                for l2, h2, m, w2 in hist.get(name, ()):
                    if wr and w2 and o["rows"] and ops[m]["rows"] not in (False, o["rows"]):
                        continue
                    if (ps and (ops[m]["q"] != o["q"] or o["q"] == "p")) or ((wr or w2) and l2 < hi and lo < h2):
                        deps.add(m)
        out.append(deps)
        for acc, wr in ((o["r"], False), (o["w"], True)):
            for name, lo, hi in acc:
                h = hist.setdefault(name, [])
                if wr and not o["rows"]:
                    ps = SCRATCH[name][0] == "psum"
                    h[:] = [e for e in h if (ps and ops[e[2]]["q"] != o["q"]) or not (lo <= e[0] and e[1] <= hi)]
                elif wr:
                    h[:] = [e for e in h if ops[e[2]]["rows"] != o["rows"]]
                h.append((lo, hi, n, wr))
    return out


def arrange(ops):
    pre = conflicts(ops)
    lastkey = {}
    suc = [[] for _ in ops]
    for n, o in enumerate(ops):
        lastkey[o["key"]] = n
        if o["xw"]:
            pre[n].add(lastkey["snt"])
    for q in "vspgy":
        line = sorted((o["place"], n) for n, o in enumerate(ops) if o["q"] == q)
        for (_, m), (_, n) in zip(line, line[1:]):
            pre[n].add(m)
    for n, p in enumerate(pre):
        for m in p:
            suc[m].append(n)
    left = [len(p) for p in pre]
    order = [n for n in range(len(ops)) if left[n] == 0]
    for n in order:
        for s in suc[n]:
            left[s] -= 1
            if left[s] == 0:
                order.append(s)
    assert len(order) == len(ops)
    return order


def plan(ops):
    known = {}
    newest = {}
    for n, (o, deps) in enumerate(zip(ops, conflicts(ops))):
        kn = known.setdefault(o["q"], {})
        best = {}
        for m in deps:
            key = ops[m]["key"]
            if key == "qp" == o["key"]:
                continue
            if ops[m]["dma"] and kn.get(key, -1) < m:
                m = newest[key]
            if m > best.get(key, -1):
                best[key] = m
        waits = []
        for key, m in sorted(best.items(), key=lambda e: -e[1]):
            if kn.get(key, -1) >= m:
                continue
            waits.append(m)
            for k2, m2 in ops[m]["clock"].items():
                if kn.get(k2, -1) < m2:
                    kn[k2] = m2
        o["waits"] = waits
        o["clock"] = dict(kn)
        o["clock"][o["key"]] = n
        for m in waits:
            ops[m]["sig"] = True
        if o["dma"]:
            newest[o["key"]] = n


def rank_program(g, core, T, topo):
    rank = T.rank_of(core)
    if rank is None:
        return
    AL, AF = AluOpType, ActivationFunctionType
    eng = {"v": g.vector, "s": g.scalar, "p": g.tensor, "g": g, "y": g.sync}
    ops = []
    now = [0, "pro"]

    def at(name):
        now[1] = name

    def ap(x):
        if not isinstance(x, tuple):
            return x
        if isinstance(x[0], tuple):
            return ap(x[0]).indirect(ap(x[1]))
        if len(x) == 4:
            return T[x[0]][:, x[1]:x[2]:x[3]]
        return T[x[0]][:, x[1]:x[2]]

    def regs(xs):
        out = []
        for x in xs:
            if isinstance(x, tuple):
                out += regs(x) if isinstance(x[0], tuple) else [x[:3]]
        return out

    def put(q, fn, r, w, xw=(), sem=None, inc=0, rows=False):
        names = OPT["first" if now[0] == 0 else "last" if now[0] == RO - 1 else "later"][q].split()
        ops.append({"q": q, "fn": fn, "r": regs(r), "w": regs(w), "xw": list(xw), "dma": sem is not None, "inc": inc,
                    "key": sem if sem is not None else QSEM[q], "sig": False, "rows": rows,
                    "place": (now[0], names.index(now[1]))})

    def ts(out, in0, s1, s2, op0, op1=None):
        if op1 is None:
            put("v", lambda e: e.tensor_scalar(ap(out), ap(in0), ap(s1), None, op0), [in0, s1], [out])
        else:
            put("v", lambda e: e.tensor_scalar(ap(out), ap(in0), ap(s1), ap(s2), op0, op1), [in0, s1, s2], [out])

    def tt(out, in0, in1, op, xw=()):
        put("v", lambda e: e.tensor_tensor(ap(out), ap(in0), ap(in1), op), [in0, in1], [out], xw)

    def cp(out, in_):
        put("v", lambda e: e.tensor_copy(ap(out), ap(in_)), [in_], [out])

    def fill(out, c):
        put("v", lambda e: e.memset(ap(out), c), [], [out])

    def act(out, in_, func, bias=0.0, scale=1.0):
        put("s", lambda e: e.activation(ap(out), ap(in_), func, bias=bias, scale=ap(scale)), [in_, scale], [out])

    def mms(calls):
        def fn(e):
            return [e.matmul(ap(o), ap(lt), ap(rh), a, b) for o, lt, rh, a, b in calls][-1]
        put("p", fn, [c[1] for c in calls] + [c[2] for c in calls], [c[0] for c in calls])

    def grp(terms, start=True, stop=True):
        mms([c + (start and k == 0, stop and k == len(terms) - 1) for k, c in enumerate(terms)])

    def mm(out, terms, start=True, stop=True):
        grp([(out, lt, rh) for lt, rh in terms], start, stop)

    def iota(out, pattern, mult, flag=True):
        if flag:
            put("g", lambda e: e.iota(ap(out), pattern, 0, mult, allow_small_or_imprecise_dtypes=True), [], [out])
        else:
            put("g", lambda e: e.iota(ap(out), pattern, 0, mult), [], [out])

    def dmas(q, sem, pairs, r, w, add=False, rows=False):
        def fn(e):
            for o, i in pairs:
                (e.dma_start(o, i, accum_op=AL.add) if add else e.dma_start(o, i)).then_inc(T.sem[sem], 16)
        put(q, fn, r, w, (), sem, 16 * len(pairs), rows)

    def turned(sb, hb, step):
        out = []
        n = 16 // step
        for h0, h1, g0 in ((0, NR - rank, rank), (NR - rank, NR, 0)):
            if h1 > h0:
                out.append((sb(slice(16 * h0, 16 * h1, step)), hb(slice(n * g0, n * (g0 + h1 - h0)))))
        return out

    def idm(scale):
        k = SCALES.index(scale)
        return ("ids", 128 * k, 128 * k + 128)

    def cn(i, name="cb"):
        return (name, 15 - i, 143 - i)

    def join(bank, col, scale, name, h=None, base=0):
        a, n = (0, 128) if h is None else (64 * h, 64)
        return [((bank, col + 2 * a + p, col + 2 * a + 2 * n, 2), idm(scale),
                 (name, base + PITCH * p + a, base + PITCH * p + a + n)) for p in range(2)]

    def split(bank, scale, name):
        lt = idm(scale) if isinstance(scale, float) else scale
        return [((bank, PITCH * p, PITCH * p + 128), lt, (name, p, 256, 2)) for p in range(2)]

    def whole(bank, scale, name):
        return [((bank, 0, SW), idm(scale), (name, 0, SW))]

    def back(bank, q, h, col=0):
        return [((bank, col + 128 * h, col + 128 * h + 128), ("ts", 512 * h + 128 * q, 512 * h + 128 * q + 128), idm(1.0))]

    def backs(bank, q, scale=1.0):
        _, a, b = idm(scale)
        return [((bank, PITCH * p + 64 * h, PITCH * p + 64 * h + 64), ("ts", 512 * h + 128 * q, 512 * h + 128 * q + 128),
                 ("ids", a + p, b, 2)) for h in range(2) for p in range(2)]

    far = [d for d in range(1, NR) if topo.chip(T.cores[(rank + d) % NR]) != topo.chip(core)]
    near = [d for d in range(1, NR) if d not in far]
    fmask = topo.mask(core, T.cores[(rank + far[0]) % NR])
    nmask = topo.mask(core, T.cores[(rank + near[0]) % NR]) & ~fmask
    nf, nn = bin(fmask).count("1"), bin(nmask).count("1")
    arrive = nf * len(far) + nn * len(near)

    def send(x, t):
        def dst(d):
            rid, pid, _ = topo.addr(T.cores[(rank + d) % NR])
            return DstId(rid=rid, pnc=pid)

        def fn(e):
            tr = [RemoteDMATransfer(dst_ids=[dst(d) for d in ds], dma_engine_mask=m, remote_sem=T.sem["arr%d" % t],
                                    srcs=[T[x][:, 0:GH]], dsts=[T[x][:, V + (d - 1) * GH:V + d * GH] for d in ds])
                  for ds, m in ((far, fmask), (near, nmask))]
            e.remote_dma_fused(tr, local_sem=T.sem["snt"])
        put("g", fn, [(x, 0, GH)], [], (), "snt", nf + nn)

    def spread(q, name, sem, base=0):
        dmas("y", sem, [(T.mw[q:128:16, 16 * PITCH * p:16 * PITCH * (p + 1)],
                         T[name][:, base + PITCH * p:base + PITCH * (p + 1)]) for p in range(2)],
             [(name, base, base + 2 * PITCH)], [("mw", 0, MW)], rows=q + 1)

    dmas("y", "lgh", turned(lambda p: T.xa[p, 0:GH], lambda p: T.x0[p, 0:GH], 1), [], [("xa", 0, GH)])
    dmas("s", "lad", turned(lambda p: T.adi[p, :], lambda p: T.ad[p, :], 1), [], [("adi", 0, 256)])
    fill(("sgi", 0, 276), 0)
    fill(("lmi", 0, 276), 0)
    dmas("y", "lx", turned(lambda p: T.xa[p, GH:V], lambda p: T.x0[p, GH:V], 1), [], [("xa", GH, V)])
    dmas("s", "ltb", turned(lambda p: T.sgi[p, 0:273], lambda p: T.sg[p, :], 16)
         + turned(lambda p: T.lmi[p, 0:273], lambda p: T.lm[p, :], 16), [], [("sgi", 0, 276), ("lmi", 0, 276)])
    iota(("pi", 0, 1), [[0, 1]], 1, False)
    iota(("colf", 0, 144), [[1, 144]], 0)
    iota(("colb", 0, 128), [[16, 8], [0, 16]], 0)
    send("xa", 0)
    for k in range(1, 4):
        dmas("y", "own%d" % k, turned(lambda p: T.own[p, CH * k:CH * k + CH], lambda p: T.x0[p, CH * k:CH * k + CH], 1),
             [("xa", GH, V)], [("own", CH * k, CH * k + CH)])
    for k in range(4):
        a = 2 * CH * k + CH
        dmas("y", "lxi%d" % k, turned(lambda p: T.wn[p, a:a + CH], lambda p: T.xi[p, CH * k:CH * k + CH], 1),
             [], [("wn", a, a + CH)])
    iota(("seli", 0, 32), [[1, 4], [16, 8]], 0)
    iota(("stab", 0, 256), [[0, 4], [1, 64]], 0)
    P, PB, PM, PO, NF, L0, L1 = [("pc", k, k + 1) for k in range(7)]
    BO, FM, I1 = ("bo", 0, 128), ("fm", 0, 128), idm(1.0)
    ts(("pi", 1, 2), ("pi", 0, 1), 112, None, AL.bitwise_and)
    cp(("pc", 0, 2), ("pi", 0, 2))
    tt(PM, P, PB, AL.subtract)
    ts(idm(1.0), ("colf", 0, 128), P, None, AL.is_equal)
    ts(("cb", 0, 144), ("colf", 0, 144), PB, 15.0, AL.subtract, AL.is_equal)
    ts(BO, ("colb", 0, 128), PB, None, AL.is_equal)
    ts(("f1", 0, 128), ("colf", 0, 128), P, 16.0, AL.is_gt, AL.mult)
    ts(("mk", 0, 16), ("colf", 0, 16), PM, 256.0, AL.is_equal, AL.mult)
    ts(PO, PM, float(CH), None, AL.add)
    ts(("ch", 0, 144), ("cb", 0, 144), 0.5, None, AL.mult)
    ts(NF, PM, 0.0, -1.0, AL.is_equal, AL.mult)
    ts(L0, PM, -8.0, -1.0, AL.mult, AL.add)
    ts(L1, PM, -8.0, -129.0, AL.mult, AL.add)
    ts(("f2", 0, 128), idm(1.0), 255.0, 1.0, AL.mult, AL.add)
    fill(("ones", 0, 128), 1.0)
    fill(("c128", 0, 64), 128.0)
    fill(("z16", 0, 16), 0.0)
    tt(("f1", 0, 128), ("f1", 0, 128), ("f2", 0, 128), AL.add)
    cp(("off", 0, 256), ("adi", 0, 256))
    tt(FM, ("f1", 0, 128), BO, AL.mult)
    ts(("ahi", 0, 256), ("adi", 0, 256), 5, None, AL.arith_shift_right)
    ts(("ali", 0, 256), ("adi", 0, 256), 31, None, AL.bitwise_and)
    ts(("ia0", 0, 256), ("off", 0, 256), float(V), -6.0, AL.is_lt, AL.mult)
    ts(("q0", 0, 256), ("ali", 0, 256), -192.0, None, AL.add)
    cp(("h0", 0, 256), ("ahi", 0, 256))
    at("ids")
    for s in SCALES[1:]:
        act(idm(s), idm(1.0), AF.Identity, 0.0, s)
    for t in range(16):
        at("bc%d" % (t // 8))
        act(("bc", 128 * t, 128 * t + 128), BO, AF.Identity, 0.0, ("mk", t, t + 1))
    at("kl")
    fill(("kl", 0, SW), -1536.0)
    fill(("dh", 0, SW), 0.0)
    fill(("dl", 0, SW), 0.0)
    fill(("dq", 0, SW), 192.0)
    fill(("gr", 0, 2 * PITCH), -5.0)
    fill(("nb", 0, 2 * PITCH * RO), 1.0)
    fill(("k1", 16, 17), 0.0)
    fill(("k1", 17, 32), 1.0)
    for name, c in (("hs", 0.0), ("ls", -1536.0), ("nts", 0.0)):
        fill((name, 128, PITCH), c)
    fill(("uh", SW, 2 * PITCH), 0.0)
    fill(("ul", SW, 2 * PITCH), 0.0)
    for p, own in enumerate((L0, L1)):
        a, b = PITCH * p, PITCH * p + 128
        fill(("gr", a, b), 1.0)
        act(("hs", a, b), ("colf", 0, 128), AF.Identity, 0.0, -1.0)
        act(("ls", a, b), ("ones", 0, 128), AF.Identity, 0.0, own)
    at("ks")
    ts(("sel", 0, 32), ("seli", 0, 32), P, None, AL.is_equal)
    ts(("se3", 0, 8), ("sel", 24, 32), -512.0, None, AL.mult)
    ts(("se3", 8, 16), ("sel", 24, 32), -512.0, None, AL.mult)
    ts(("se3", 16, 24), ("seli", 16, 24), P, None, AL.is_le)
    ts(("sel", 16, 24), ("seli", 16, 24), 5.0, P, AL.add, AL.is_ge)
    tt(("sel", 0, 16), ("sel", 0, 16), ("se3", 0, 16), AL.add)
    tt(("sel", 16, 24), ("sel", 16, 24), ("se3", 16, 24), AL.mult)
    at("km")
    mm(("p1", 0, 256), [(idm(float(PITCH)), ("q0", 0, 256)), (I1, ("h0", 0, 256))])
    ts(("off", 256, 512), ("p1", 0, 256), 192.0 * PITCH, None, AL.add)
    at("kt")
    ts(("e0", 0, 276), ("sgi", 0, 276), -239.5, 256.0, AL.mult, AL.add)
    ts(("nlm", 0, 276), ("lmi", 0, 276), 1.0, NF, AL.add, AL.mult)
    ts(("nth", 0, 276), ("e0", 0, 276), 1.0, NF, AL.max, AL.mult)
    mm(("p5", 0, 16), [(cn(t), ("nlm", t, 256, 16)) for t in range(16)])
    mm(("p5", 16, 17), [(BO, ("nlm", 272, 273))])
    mm(("p5", 17, 18), [(BO, ("nth", 272, 273))])
    mms([(("p5", a, a + 16), BO, (name, 256, 272), True, True) for a, name in ((24, "nlm"), (40, "nlm"), (56, "nth"))])
    for k in range(MW // CH):
        at("mw%d" % k)
        act(("mw", CH * k, CH * k + CH), ("ids", 0, CH), AF.Identity, 1.0, 0.0)
    at("own")
    cp(("own", 0, CH), ("xa", 0, CH))
    at("late")
    for p in range(2):
        act(("nts", PITCH * p, PITCH * p + 128), ("nth", p, 256, 2), AF.Identity)
    ts(("tbl", 0, 18), ("p5", 0, 18), -1.0, -1.0, AL.mult, AL.add)
    ts(("tbl", 24, 72), ("p5", 24, 72), -1.0, None, AL.mult)
    ts(("k1", 0, 16), ("z16", 0, 16), ("tbl", 17, 18), 16.0, AL.add, AL.is_le)
    tt(("tbl", 17, 18), ("tbl", 16, 17), ("tbl", 17, 18), AL.min)

    for t in range(RO):
        cur, nxt = ("xa", "xb") if t % 2 == 0 else ("xb", "xa")
        first, last = t == 0, t == RO - 1
        o = 0 if first else 2 if last else 1
        now[0] = t
        nb = 2 * PITCH * t
        NB = ("nb", nb, nb + SW)

        if not first:
            for h in range(2):
                for k in (2 * h, 2 * h + 1):
                    at("m%d" % k)
                    act(("mg", CH * k, CH * k + CH), (("mw", 0, MW), ("off", 256 + 64 * k, 320 + 64 * k)), AF.Identity)
                at("T%d" % h)
                mms([(("p%d" % h, i, 512, 16), ("mg", 2048 * h + i, 2048 * h + 2048, 16), ("sel", 0, 32), True, True)
                     for i in range(16)])
                at("ts%d" % h)
                act(("ts", 512 * h + 256, 512 * h + 512), ("p%d" % h, 256, 512), AF.Identity, 1.0, -1.0)
                at("tv%d" % h)
                ts(("ts", 512 * h, 512 * h + 256), ("p%d" % h, 0, 256), 512.0, 256.0, AL.add, AL.min)
            for h in range(2):
                at("sp%d" % h)
                grp(back("p3", 2, h) + join("p3", 0, -1.0, "dl", h) + join("p3", 0, 8.0, "dq", h))
            at("st")
            act(("st", 0, 256), ("p3", 0, 256), AF.Relu, -16.0 * 1537, 16.0)
        cuts = OPT["cuts"]
        for k, (a, b) in enumerate(zip(cuts, cuts[1:])):
            at("g%d" % k)
            tt(("dd", a, b), ((cur, 0, WX), ("off", a // 16, b // 16)), ("own", a, b), AL.subtract,
               [("arr%d" % t, arrive)] if k == 0 else [])
            if k > 0:
                ops[-1]["r"].append(("dd", 0, 1))
            at("c%d" % k)
            if (OPT["cmp"][o] + "v")[k] == "s":
                act(("cm", a, b), ("dd", a, b), AF.Sign, 12.5)
                at("n%d" % k)
                mm(("p2", a // 16, b // 16), [(idm(3.0 / 128), ("c128", 0, (b - a) // 16))]
                   + [(cn(i, "ch"), ("cm", a + i, b, 16)) for i in range(16)])
            else:
                ts(("cm", a, b), ("dd", a, b), -12.5, -0.3125, AL.is_gt, AL.add)
                at("n%d" % k)
                mm(("p2", a // 16, b // 16), [(cn(i), ("cm", a + i, b, 16)) for i in range(16)])
        if not last:
            at("wi")
            if first:
                spread(2, "gr", "lmw")
            else:
                spread(3 + t, "nb", "lmw", nb - 2 * PITCH)
            at("pu")
            grp(whole("p0", 1.0, "hs") + whole("p0", 1.0, "dh") + split("p0", 1.0, "h0"))
            at("pv")
            grp(whole("p1", 1.0, "ls") + whole("p1", 8.0, "dq") + split("p1", 8.0, "q0")
                + (split("p1", 1.0, "ia0") + [(("p1", PITCH * p, PITCH * p + 128), I1, ("ones", 0, 128)) for p in range(2)]
                   if first else backs("p1", 2)))
            for q, (name, bank) in enumerate((("uh", "p0"), ("ul", "p1"))):
                at(name)
                act((name, 0, SW), (bank, 0, SW), AF.Identity)
                at("w" + name[1])
                spread(q, name, "lmw")
        banks = ["p" + c for c in OPT["banks"][o]]
        bank = 0
        for k in range(4):
            for u in (2 * k, 2 * k + 1):
                a = 512 * u
                m = ("wn", a + CH * k, a + CH * k + 512)
                at("r%d" % u)
                if OPT["add"][o][k] == "q":
                    pb = (banks[bank % len(banks)], 0, 512)
                    bank += 1
                    at("x%d" % u)
                    mm(pb, [(I1, (cur, a, a + 512))], True, False)
                    at("y%d" % u)
                    mm(pb, [(I1, ("dd", a, a + 512))], False, True)
                    at("e%d" % u)
                    tt(m, pb, ("own", a, a + 512), AL.max)
                elif OPT["relu"][o][u] == "v":
                    ts(m, ("dd", a, a + 512), 0.0, None, AL.max)
                else:
                    act(m, ("dd", a, a + 512), AF.Relu)
                if OPT["add"][o][k] == "p":
                    pb = (banks[bank % len(banks)], 0, 512)
                    bank += 1
                    at("x%d" % u)
                    mm(pb, [(I1, (cur, a, a + 512))], True, False)
                    at("y%d" % u)
                    mm(pb, [(I1, m)], False, True)
                    at("e%d" % u)
                    act(m, pb, AF.Identity)
            if OPT["add"][o][k] == "d":
                a, m = CH * k, ("wn", 2 * CH * k, 2 * CH * k + CH)
                at("a%d" % k)
                dmas("g", "acc%d" % k, [(ap(m), ap((cur, a, a + CH)))], [(cur, a, a + CH), m], [m], True)
        if not first:
            at("pa")
            grp(whole("p3", 1.0, "dh") + backs("p3", 0) + backs("p3", 3, -256.0))
            at("pl")
            grp(whole("p6", 8.0, "dq") + whole("p6", 1.0, "kl") + backs("p6", 1) + backs("p6", 3, -256.0))
        if last:
            at("g7")
            ts(("g7", 0, 256), ("off", 0, 256), float(V), -7.0, AL.is_ge, AL.mult)
            at("po")
            grp([(("p2", 256, 512), idm(512.0), ("h0", 0, 256)), (("p2", 256, 512), idm(16.0), ("q0", 0, 256)),
                 (("p2", 256, 512), I1, ("g7", 0, 256))] + join("p2", 256, 512.0, "dh") + join("p2", 256, 16.0, "dq")
                + back("p2", 2, 0, 256) + back("p2", 2, 1, 256), True, False)
        fast = OPT["fast"] and not last
        at("j0")
        mm(("p4", 0, SW), [(BO, ("nts", 0, SW))], True, False)
        at("o0")
        mm(("p7", 0, 256), [(idm(16.0), ("stab", 0, 256))], True, False)
        c = cuts[-2] // 16 if OPT["crs"] else 0
        for name, a, b in (("cq", 0, c), ("cr", c, 256)):
            at(name)
            if a == b:
                continue
            if first:
                ts(("cr", a, b), ("p2", a, b), 0.0, None, AL.is_le)
            else:
                tt(("cr", a, b), ("p2", a, b), ("st", a, b), AL.is_le)
        at("j1")
        mm(("p5", 0, 16), [(cn(k), ("cr", k, 256, 16)) for k in range(16)])
        at("j2")
        grp(split("p4", FM, "cr"), False, False)
        if fast:
            at("h0")
            mm(("p2", 256, 264), [(BO, ("nth", 0, 8)), (FM, ("cr", 0, 8))], True, False)
        at("d1")
        tt(("d1", 0, 16), ("p5", 0, 16), ("tbl", 0, 16), AL.is_gt)
        at("j3")
        mms([(("p5", a, a + 16), lt, ("d1", 0, 16), True, True) for a, lt in ((16, BO), (32, BO), (48, FM))])
        at("db")
        tt(("db", 0, 48), ("p5", 16, 64), ("tbl", 24, 72), AL.is_ge)
        at("sc")
        put("v", lambda e: e.tensor_tensor_scan(T.us[:, 0:32], T.k1[:, 0:32], T.db[:, 0:32], 0.0, AL.mult, AL.add),
            [("k1", 0, 32), ("db", 0, 32)], [("us", 0, 32)])
        at("zz")
        tt(("zz", 0, 16), ("us", 0, 16), ("db", 32, 48), AL.max)
        at("d3")
        ts(("d3", 0, 2), ("tbl", 16, 18), ("us", 31, 32), -0.25, AL.is_lt, AL.add)
        if fast:
            at("h1")
            grp([(("p2", 256 + k, 257 + k), ("bc", 128 * k, 128 * k + 128), ("zz", 0, 1)) for k in range(8)], False, True)
        at("j4")
        grp([(("p4", PITCH * (k % 2) + k // 2, PITCH * (k % 2) + 128, 8), ("bc", 128 * k, 128 * k + 128), ("zz", 0, 16))
             for k in range(16)], False, True)
        at("j5")
        mm(("p5", 64, 65), [(("ones", 0, 128), ("d3", 0, 1)), (idm(64.0), ("d3", 1, 2))])
        if fast:
            at("nbg")
            ts(("nbg", 0, 8), ("p2", 256, 264), ("p5", 64, 65), 0.0, AL.max, AL.is_lt)
            at("h2")
            mm(("p2", 272, 280), [(idm(16.0), ("stab", 0, 8)), (idm(-1024.0), ("nbg", 0, 8))])
            at("offg")
            ts(("offg", 0, 8), ("p2", 272, 280), PO, None, AL.add)
        at("nb")
        for a in (0, PITCH):
            ts(("nb", nb + a, nb + a + 128), ("p4", a, a + 128), ("p5", 64, 65), 0.0, AL.max, AL.is_lt)
        at("o1")
        grp(join("p7", 0, -1024.0, "nb", None, nb), False, True)
        at("offs")
        ts(("offs", 0, 256), ("p7", 0, 256), PO, None, AL.add)

        def pick(q, a, b, off="offs"):
            k = a // CH
            src = (("wn", 2 * CH * k, 2 * CH * k + 2 * CH), (off, a // 16, b // 16))
            if q == "v":
                cp((nxt, a, b), src)
            else:
                act((nxt, a, b), src, AF.Identity)

        def result(y, src, a, b, sem):
            dmas("y", sem, [(o, i) for i, o in turned(lambda p: T[src][p, a:b], lambda p: y[p, a:b], 1)], [(src, a, b)], [])

        if not last:
            at("gp")
            pick("v", 0, GH, "offg" if fast else "offs")
            at("send")
            send(nxt, t + 1)
            at("wn")
            spread(3, "nb", "lmn", nb)
        else:
            at("pi")
            for p in range(2):
                grp([join("p4", 0, -1.0, "nb", None, 2 * PITCH * k)[p] for k in range(RO)])
            at("inc")
            act(("oi", 0, 256), ("p4", 0, 256), AF.Identity, RO + 1.0)
            result(T.yi, "oi", 0, 256, "ol")
            at("ou1")
            grp(join("p2", 256, BIG, "nb", None, nb), False, True)
            at("ou")
            ts(("ou", 0, 256), ("p2", 256, 512), 6.0 - BIG, -1.0, AL.add, AL.max)
            result(T.yu, "ou", 0, 256, "ol")
        if not first:
            at("dl")
            tt(("dl", 0, SW), ("p6", 0, SW), NB, AL.mult)
            at("dh")
            tt(("dh", 0, SW), ("p3", 0, SW), NB, AL.mult)
            at("dq")
            if OPT["dq"] == "v":
                ts(("dq", 0, SW), ("dl", 0, SW), 0.125, 192.375, AL.mult, AL.add)
            else:
                act(("dq", 0, SW), ("dl", 0, SW), AF.Identity, 192.375, 0.125)
        if last:
            at("f1")
            for p in range(2):
                grp([join("p1", 0, 1.0, "dl")[p], join("p1", 0, -8.0, "dq")[p]])
            at("f7")
            ts(("f7", 0, 256), ("p1", 0, 256), -1536.0, -7.0, AL.is_equal, AL.mult)
            at("oa1")
            grp([(("p2", 0, 256), idm(512.0), ("h0", 0, 256)), (("p2", 0, 256), idm(16.0), ("q0", 0, 256))]
                + join("p2", 0, 512.0, "dh") + join("p2", 0, 8.0, "dq") + join("p2", 0, 1.0, "dl")
                + [(("p2", 0, 256), I1, ("f7", 0, 256))])
            at("oa2")
            ts(("oa", 0, 256), ("p2", 0, 256), 1543.0, None, AL.add)
            result(T.ya, "oa", 0, 256, "ol")
        elif not first:
            at("om")
            grp([(("p2", 256, 512), I1, ("h0", 0, 256)), (("p2", 256, 512), idm(float(PITCH)), ("q0", 0, 256))]
                + join("p2", 256, 1.0, "dh") + join("p2", 256, float(PITCH), "dq"))
            at("oa")
            grp([(("p2", 0, 256), idm(32.0), ("h0", 0, 256)), (("p2", 0, 256), I1, ("q0", 0, 256))]
                + join("p2", 0, 32.0, "dh") + join("p2", 0, 1.0, "dq"))
            at("off")
            cp(("off", 0, 512), ("p2", 0, 512))
        vs = OPT["vsel"][t]
        for q, a, end, most in (("s", 0 if last else GH, V - vs, 768 if last else CH), ("v", V - vs, V, OPT["piece"])):
            n = 0
            while a < end:
                b = min((a // most + 1) * most if q == "v" else a + most, end, (a // CH + 1) * CH)
                at(q + str(min(n, 3 if q == "v" or last else 2)))
                pick(q, a, b)
                if last:
                    result(T.yx, nxt, a, b, "oy")
                a = b
                n += 1
        for k in range(0 if last else 4):
            a, b = CH * k, CH * k + CH
            at("w%d" % k)
            if OPT["own"][k] == "v":
                cp(("own", a, b), (nxt, a, b))
            elif OPT["own"][k] == "s":
                act(("own", a, b), (nxt, a, b), AF.Identity)
            else:
                dmas("y", "own%d" % k, [(T.own[:, a:b], T[nxt][:, a:b])], [(nxt, a, b)], [("own", a, b)])

    ops = [ops[n] for n in arrange(ops)]
    plan(ops)
    total = {}
    for o in ops:
        if o["dma"]:
            total[o["key"]] = total.get(o["key"], 0) + o["inc"]
        elif o["sig"]:
            total[o["key"]] = total.get(o["key"], 0) + 1
        o["val"] = total.get(o["key"], 0)
    for o in ops:
        e = eng[o["q"]]
        for m in o["waits"]:
            e.wait_ge(T.sem[ops[m]["key"]], ops[m]["val"])
        for s, v in o["xw"]:
            e.wait_ge(T.sem[s], v)
        ins = o["fn"](e)
        if o["sig"] and not o["dma"]:
            ins.then_inc(T.sem[o["key"]], 1)
    g.sync.wait_ge(T.sem["oy"], total["oy"])
    g.sync.wait_ge(T.sem["ol"], total["ol"])
    g.wait_ge(T.sem["snt"], total["snt"])
